import numpy as np
import ml_dtypes


def mxq(x, axis, fmt="e4m3"):
    dtype, down = {"e4m3": (ml_dtypes.float8_e4m3fn, 7), "e5m2": (ml_dtypes.float8_e5m2, 14)}[fmt]
    v = np.moveaxis(np.asarray(x, np.float32).astype(ml_dtypes.bfloat16).astype(np.float64), axis, -1)
    blocks = v.reshape(v.shape[:-1] + (-1, 32))
    amax = np.abs(blocks).max(-1, keepdims=True)
    byte = np.maximum(np.where(amax > 0, np.frexp(amax)[1] - 1 + 127, 0) - down, 1)
    scale = np.exp2(byte - 127.0)
    codes = (blocks / scale).astype(np.float32).astype(dtype).astype(np.float64)
    return np.moveaxis((codes * scale).reshape(v.shape), -1, axis)


WIDE = False


def mx_kscale(k):
    if not WIDE:
        return np.ones(k)
    levels = np.array([10, -10, 5, -5, 0])
    if k % 512:
        return np.exp2(np.random.permutation(np.resize(levels, k // 32))).repeat(32)
    a = np.empty((k // 512, 16))
    for p in range(k // 512):
        a[p, :8] = np.random.permutation(np.resize(levels, 8))
        for g in range(8):
            far = levels[np.abs(levels - a[p, g]) >= 10]
            a[p, g + 8] = far[np.random.randint(len(far))]
    return np.exp2(a.ravel()).repeat(32)


def f64(x):
    return np.asarray(x).astype(np.float64)


def striped(idx):
    return np.tile(idx.reshape(-1, 16).T, (8, 1)).astype(np.uint16)


def unstriped(offs):
    return offs[:16].T.reshape(-1).astype(np.int64)


def striped8(idx):
    return np.concatenate([x.reshape(-1, 16).T for x in idx]).astype(np.uint16)


def runs(offs, k):
    lists = np.stack([offs[16 * r : 16 * r + 16].T.reshape(-1) for r in range(8)]).astype(np.int64)
    return lists[np.arange(k) % 512 // 64]


def pack_weight(w):
    k, n = w.shape
    w = f64(np.asarray(w, np.float32).astype(ml_dtypes.bfloat16)).reshape(k // 32, 32, n)
    amax = np.abs(w).max(1)
    byte = np.clip(np.where(amax > 0, np.frexp(amax)[1] - 1 + 127 - 7, 1), 1, 254)
    scaled = (w * np.exp2(127.0 - byte)[:, None, :]).reshape(k, n).astype(np.float32)
    words = np.ascontiguousarray(scaled.reshape(k // 512, 128, 4, n).transpose(0, 1, 3, 2)).astype(ml_dtypes.float8_e4m3fn).view(np.uint8)
    return words, np.ascontiguousarray(byte.astype(np.uint8).reshape(k // 512, 16, n))


def unpack_weight(words, scales):
    g, p, n, _ = words.shape
    vals = np.ascontiguousarray(words).view(ml_dtypes.float8_e4m3fn).astype(np.float64) * np.repeat(np.exp2(scales.astype(np.float64) - 127.0), 8, axis=1)[..., None]
    return vals.transpose(0, 1, 3, 2).reshape(g * 512, n)


E2M1 = np.array([0.0, 0.5, 1.0, 1.5, 2.0, 3.0, 4.0, 6.0, -0.0, -0.5, -1.0, -1.5, -2.0, -3.0, -4.0, -6.0])


def pack_fp4(w):
    k, n = w.shape
    w = f64(np.asarray(w, np.float32).astype(ml_dtypes.bfloat16)).reshape(k // 32, 32, n)
    amax = np.abs(w).max(1)
    mant, ex = np.frexp(amax / 6.0)
    byte = np.clip(np.where(amax > 0, np.where(mant > 0.5, ex, ex - 1) + 127, 1), 1, 254)
    scaled = (w * np.exp2(127.0 - byte)[:, None, :]).reshape(k, n).astype(np.float32)
    c = np.ascontiguousarray(scaled.reshape(k // 512, 128, 4, n).transpose(0, 1, 3, 2)).astype(ml_dtypes.float4_e2m1fn).view(np.uint8) & 0xF
    words = (c[..., 0::2] | (c[..., 1::2] << 4)).reshape(k // 512, 128, 2 * n)
    return np.ascontiguousarray(words), np.ascontiguousarray(byte.astype(np.uint8).reshape(k // 512, 16, n))


def unpack_fp4(words, scales):
    g, _, n = scales.shape
    words = np.ascontiguousarray(words).reshape(g, 128, n, 2)
    nib = np.empty((g, 128, n, 4), np.uint8)
    nib[..., 0::2] = words & 0xF
    nib[..., 1::2] = words >> 4
    vals = E2M1[nib] * np.repeat(np.exp2(scales.astype(np.float64) - 127.0), 8, axis=1)[..., None]
    return vals.transpose(0, 1, 3, 2).reshape(g * 512, n)


def planes(y):
    n, m = y.shape
    v = y.astype(np.float32).astype(ml_dtypes.bfloat16).astype(np.float64).reshape(n // 32, 32, m)
    top = np.abs(v).max(1)
    byte = np.clip(np.where(top > 0, np.frexp(top)[1] - 1 + 127 - 7, 1), 1, 254)
    codes = (v * np.exp2(127.0 - byte)[:, None, :]).reshape(n, m).astype(np.float32).astype(ml_dtypes.float8_e4m3fn).view(np.uint8)
    words = codes.reshape(n // 512, 128, 4, m).transpose(0, 1, 3, 2)
    return np.ascontiguousarray(words), np.ascontiguousarray(byte.astype(np.uint8).reshape(n // 512, 16, m))


K, T, S, N, G, H = 512, 2048, 512, 512, 2048, 512


def setup_inputs():
    n = np.random.standard_normal
    s = mx_kscale(K)[:, None]
    u = mx_kscale(H)
    packed_xT = pack_weight(n((K, T)) * s)
    packed_dT = pack_weight(n((K, G)) / s)
    packed_w1 = pack_fp4(n((H, N)) / np.sqrt(H) / u[:, None])
    return {
        "x_words": packed_xT[0],
        "x_scales": packed_xT[1],
        "d_words": packed_dT[0],
        "d_scales": packed_dT[1],
        "gn": (np.random.uniform(0.5, 1.5, (H, 1)) * u[:, None]).astype(np.float32),
        "w1_words": packed_w1[0],
        "w1_scales": packed_w1[1],
        "offs": striped(np.random.permutation(T)[:S]),
        "kidx": striped8(np.random.randint(0, G, (8, H))),
        "nb": striped8(np.stack([np.random.permutation(S) for _ in range(8)])),
    }


def reference(x_words, x_scales, d_words, d_scales, gn, w1_words, w1_scales, offs, kidx, nb):
    d_kidx = unpack_weight(d_words, d_scales)[np.arange(K)[:, None], runs(kidx, K)]
    xq = unpack_weight(x_words, x_scales)[:, unstriped(offs)]
    s = 0.03125 * (d_kidx.T @ xq)
    e = np.exp(s - s.max(axis=1, keepdims=True))
    p = e / e.sum(axis=1, keepdims=True)
    z = f64(gn) * (32.0 * (p + p[np.arange(H)[:, None], runs(nb, H)]))
    out_0 = unpack_fp4(w1_words, w1_scales).T @ mxq(z, 0, "e4m3")
    return (out_0,) + planes(out_0)

@@ -1,0 +1,203 @@
+from contextlib import ExitStack
+
+import concourse.mybir as mybir
+
+F32 = mybir.dt.float32
+BF16 = mybir.dt.bfloat16
+I32 = mybir.dt.int32
+U32 = mybir.dt.uint32
+U16 = mybir.dt.uint16
+U8 = mybir.dt.uint8
+FP8X4 = mybir.dt.float8_e4m3fn_x4
+FP4X4 = mybir.dt.float4_e2m1fn_x4
+ALU = mybir.AluOpType
+ACT = mybir.ActivationFunctionType
+
+P = 128
+PACK = 4
+TABLE = 2048
+S = 512
+HALF = 256
+CHUNK = 128
+FLOPS = 2 * 2 * 512 * 512 * 512
+
+
+def tile_picked_softkeys_none_po_kernel(
+    tc, x_words, x_scales, d_words, d_scales, gn, w1_words, w1_scales, offs, kidx, nb, out_0, out_1, out_2
+):
+    nc = tc.nc
+    with ExitStack() as ctx:
+        keep = ctx.enter_context(tc.tile_pool(name="keep", bufs=1))
+        psum = ctx.enter_context(tc.psum_pool(name="psum", bufs=1))
+
+        def sb(name, shape, dtype):
+            return keep.tile(shape, dtype, name=name, align_bytes=64)
+
+        kidx_sb = sb("kidx_sb", [P, S // 16], U16)
+        offs_sb = sb("offs_sb", [P, S // 16], U16)
+        nb_sb = sb("nb_sb", [P, S // 16], U16)
+        d_tab = sb("d_tab", [P, TABLE], U32)
+        x_tab = sb("x_tab", [P, TABLE], U32)
+        ds_tab = sb("ds_tab", [P, TABLE], U8)
+        xs_tab = sb("xs_tab", [P, TABLE], U8)
+        w_raw = sb("w_raw", [P, 2 * S], U8)
+        ws_raw = sb("ws_raw", [P, S], U8)
+        gn_sb = sb("gn_sb", [P, PACK], F32)
+
+        nc.vector.memset(ds_tab[:].bitcast(I32), 0)
+        nc.vector.memset(xs_tab[:].bitcast(I32), 0)
+        nc.vector.memset(ws_raw[:].bitcast(I32), 0)
+
+        nc.sync.dma_start(kidx_sb[:], kidx)
+        nc.sync.dma_start(offs_sb[:], offs)
+        nc.sync.dma_start(nb_sb[:], nb)
+        nc.sync.dma_start(gn_sb[:], gn.rearrange("(p t) o -> p (t o)", t=PACK))
+        for e in range(2):
+            nc.sync.dma_start(ds_tab[e:P:16, :].bitcast(I32), d_scales[0][e:16:2, :].bitcast(I32))
+        nc.sync.dma_start(d_tab[:].bitcast(I32), d_words[0].rearrange("p n t -> p (n t)").bitcast(I32))
+        for q in range(4):
+            nc.sync.dma_start(xs_tab[32 * q : 32 * q + 4, :].bitcast(I32), x_scales[0][4 * q : 4 * q + 4, :].bitcast(I32))
+        nc.sync.dma_start(x_tab[:].bitcast(I32), x_words[0].rearrange("p n t -> p (n t)").bitcast(I32))
+        nc.sync.dma_start(w_raw[:].bitcast(I32), w1_words[0].bitcast(I32))
+        for q in range(4):
+            nc.sync.dma_start(ws_raw[32 * q : 32 * q + 4, :].bitcast(I32), w1_scales[0][4 * q : 4 * q + 4, :].bitcast(I32))
+
+        warm_in = sb("warm_in", [P, 1], F32)
+        warm_out = sb("warm_out", [P, 1], F32)
+        nc.vector.memset(warm_in[:], 0.0)
+        nc.scalar.activation(warm_out[:], warm_in[:], ACT.Exp)
+
+        ds_g = sb("ds_g", [P, S], U8)
+        ds_key = sb("ds_key", [P, S], U8)
+        nc.vector.tensor_copy(ds_g[:], ds_tab[:].indirect(kidx_sb[:]))
+        nc.vector.tensor_copy(
+            ds_key[:].rearrange("p (t c i) -> p c t i", t=PACK, i=16),
+            ds_g[:].rearrange("p (c i t) -> p c t i", t=PACK, i=16),
+        )
+        for e in range(2):
+            nc.scalar.dma_start(ds_key[2 + e : P : 32, :].bitcast(I32), ds_key[16 + e : P : 32, :].bitcast(I32))
+        d_g = sb("d_g", [P, S], U32)
+        d_key = sb("d_key", [P, S], U32)
+        nc.vector.tensor_copy(d_g[:], d_tab[:].indirect(kidx_sb[:]))
+        nc.vector.tensor_copy(
+            d_key[:].bitcast(I32).rearrange("p (t c i) -> p c t i", t=PACK, i=4),
+            d_g[:].bitcast(I32).rearrange("p (c i t) -> p c t i", t=PACK, i=4),
+        )
+        xs_g = sb("xs_g", [P, S], U8)
+        x_g = sb("x_g", [P, S], U32)
+        nc.vector.tensor_copy(xs_g[:], xs_tab[:].indirect(offs_sb[:]))
+        nc.vector.tensor_copy(x_g[:], x_tab[:].indirect(offs_sb[:]))
+
+        w_key = sb("w_key", [P, 2 * S], U8)
+        ws_key = sb("ws_key", [P, S], U8)
+        nc.vector.tensor_copy(
+            w_key[:].rearrange("p (t c i b) -> p c t i b", t=PACK, i=8, b=2),
+            w_raw[:].rearrange("p (c i t b) -> p c t i b", t=PACK, i=8, b=2),
+        )
+        nc.vector.tensor_copy(
+            ws_key[:].rearrange("p (t c i) -> p c t i", t=PACK, i=16),
+            ws_raw[:].rearrange("p (c i t) -> p c t i", t=PACK, i=16),
+        )
+
+        low = sb("low", [P, PACK], F32)
+        total = sb("total", [P, PACK], F32)
+        neg = [sb("neg%d" % t, [P, S], F32) for t in range(PACK)]
+        win = [sb("win%d" % t, [P, S], F32) for t in range(PACK)]
+        own = [sb("own%d" % t, [P, S], F32) for t in range(PACK)]
+        both = [sb("both%d" % t, [P, S], F32) for t in range(PACK)]
+        for t in range(PACK):
+            cols = slice(P * t, P * (t + 1))
+            score = psum.tile([P, S], F32, name="score%d" % t)
+            nc.tensor.matmul_mx(
+                out=score[:],
+                lhsT=d_key[:, cols].bitcast(FP8X4),
+                lhsT_scale=ds_key[:, cols],
+                rhs=x_g[:].bitcast(FP8X4),
+                rhs_scale=xs_g[:],
+                start=True,
+                stop=True,
+            )
+            nc.vector.tensor_scalar(neg[t][:], score[:], -0.03125, None, ALU.mult, ALU.min, accum_out=low[:, t : t + 1])
+            nc.scalar.activation(
+                win[t][:], neg[t][:], ACT.Exp, bias=low[:, t : t + 1], scale=-1.0, accum_out=total[:, t : t + 1]
+            )
+            nc.scalar.activation(own[t][:], neg[t][:], ACT.Exp, bias=low[:, t : t + 1], scale=-1.0)
+
+        def join(t, h):
+            cols = slice(HALF * h, HALF * (h + 1))
+            nc.vector.tensor_tensor(
+                both[t][:, cols], win[t][:].indirect(nb_sb[:, 16 * h : 16 * (h + 1)]), own[t][:, cols], ALU.add
+            )
+
+        inv = sb("inv", [P, PACK], F32)
+        factor = sb("factor", [P, PACK], F32)
+        z_rows = [sb("z_rows%d" % h, [P, PACK, HALF], BF16) for h in range(2)]
+        z_words = [sb("z_words%d" % h, [P, HALF * PACK], BF16) for h in range(2)]
+        z_codes = [sb("z_codes%d" % h, [P, HALF], U32) for h in range(2)]
+        z_scales = [sb("z_scales%d" % h, [P, HALF], U8) for h in range(2)]
+
+        def weigh(h):
+            for t in range(PACK):
+                nc.scalar.activation(
+                    z_rows[h][:, t, :], both[t][:, HALF * h : HALF * (h + 1)], ACT.Copy, scale=factor[:, t : t + 1]
+                )
+
+        def weave_z(h):
+            nc.vector.tensor_copy(
+                z_words[h][:].rearrange("p (c i t) -> p c t i", t=PACK, i=4),
+                z_rows[h][:].rearrange("p t (c i) -> p c t i", i=4),
+            )
+
+        def quant_z(h):
+            nc.vector.quantize_mx(out=z_codes[h][:].bitcast(FP8X4), scales=z_scales[h][:], in_=z_words[h][:])
+
+        join(0, 0)
+        join(0, 1)
+        join(1, 0)
+        join(1, 1)
+        nc.vector.reciprocal(inv[:], total[:])
+        join(2, 0)
+        nc.vector.scalar_tensor_tensor(factor[:], inv[:], 32.0, gn_sb[:], ALU.mult, ALU.mult)
+        join(3, 0)
+        weigh(0)
+        join(2, 1)
+        weave_z(0)
+        join(3, 1)
+        quant_z(0)
+        weigh(1)
+        weave_z(1)
+        quant_z(1)
+
+        y_codes = sb("y_codes", [P, S], U32)
+        y_scales = sb("y_scales", [P, S], U8)
+        out_rows = out_0.rearrange("(p t) n -> p t n", t=PACK)
+        out_codes = out_1[0].rearrange("p n t -> p (n t)").bitcast(I32)
+        for c in range(S // CHUNK):
+            h, o = divmod(CHUNK * c, HALF)
+            cols = slice(CHUNK * c, CHUNK * (c + 1))
+            acc = psum.tile([P, PACK, CHUNK], F32, name="acc%d" % c)
+            for t in range(PACK):
+                nc.tensor.matmul_mx(
+                    out=acc[:, t, :],
+                    lhsT=w_key[:, 2 * P * t : 2 * P * (t + 1)].bitcast(FP4X4),
+                    lhsT_scale=ws_key[:, P * t : P * (t + 1)],
+                    rhs=z_codes[h][:, o : o + CHUNK].bitcast(FP8X4),
+                    rhs_scale=z_scales[h][:, o : o + CHUNK],
+                    start=True,
+                    stop=True,
+                )
+            y = sb("y%d" % c, [P, PACK, CHUNK], F32)
+            nc.scalar.copy(y[:], acc[:])
+            nc.sync.dma_start(out_rows[:, :, cols], y[:])
+            y_words = sb("y_words%d" % c, [P, CHUNK * PACK], BF16)
+            nc.vector.tensor_copy(
+                y_words[:].rearrange("p (c i t) -> p c t i", t=PACK, i=4),
+                y[:].rearrange("p t (c i) -> p c t i", i=4),
+            )
+            nc.vector.quantize_mx(out=y_codes[:, cols].bitcast(FP8X4), scales=y_scales[:, cols], in_=y_words[:])
+            if c % 2 == 1:
+                pair = slice(CHUNK * (c - 1), CHUNK * (c + 1))
+                nc.sync.dma_start(out_codes[:, pair], y_codes[:, pair].bitcast(I32))
+        for q in range(4):
+            queue = nc.scalar if q % 2 == 0 else nc.sync
+            queue.dma_start(out_2[0][4 * q : 4 * q + 4, :].bitcast(I32), y_scales[32 * q : 32 * q + 4, :].bitcast(I32))

@@ -28,19 +28,22 @@ def tile_picked_softkeys_none_po_kernel(
     nc = tc.nc
     with ExitStack() as ctx:
         keep = ctx.enter_context(tc.tile_pool(name="keep", bufs=1))
+        reuse = ctx.enter_context(tc.tile_pool(name="reuse", bufs=1))
         psum = ctx.enter_context(tc.psum_pool(name="psum", bufs=1))
 
         def sb(name, shape, dtype):
             return keep.tile(shape, dtype, name=name, align_bytes=64)
 
+        def sb_at(name, shape, dtype, offset):
+            return reuse.tile(shape, dtype, name=name, align_bytes=64, offset=offset)
+
         kidx_sb = sb("kidx_sb", [P, S // 16], U16)
         offs_sb = sb("offs_sb", [P, S // 16], U16)
         nb_sb = sb("nb_sb", [P, S // 16], U16)
         d_tab = sb("d_tab", [P, TABLE], U32)
-        x_tab = sb("x_tab", [P, TABLE], U32)
+        x_tab = sb_at("x_tab", [P, TABLE], U32, 4096)
         ds_tab = sb("ds_tab", [P, TABLE], U8)
-        xs_tab = sb("xs_tab", [P, TABLE], U8)
-        w_raw = sb("w_raw", [P, 2 * S], U8)
+        xs_tab = sb_at("xs_tab", [P, TABLE], U8, 12288)
         ws_raw = sb("ws_raw", [P, S], U8)
         gn_sb = sb("gn_sb", [P, PACK], F32)
 
@@ -55,19 +58,20 @@ def tile_picked_softkeys_none_po_kernel(
         for e in range(2):
             nc.sync.dma_start(ds_tab[e:P:16, :].bitcast(I32), d_scales[0][e:16:2, :].bitcast(I32))
         nc.sync.dma_start(d_tab[:].bitcast(I32), d_words[0].rearrange("p n t -> p (n t)").bitcast(I32))
-        for q in range(4):
-            nc.sync.dma_start(xs_tab[32 * q : 32 * q + 4, :].bitcast(I32), x_scales[0][4 * q : 4 * q + 4, :].bitcast(I32))
         nc.sync.dma_start(x_tab[:].bitcast(I32), x_words[0].rearrange("p n t -> p (n t)").bitcast(I32))
-        nc.sync.dma_start(w_raw[:].bitcast(I32), w1_words[0].bitcast(I32))
         for q in range(4):
-            nc.sync.dma_start(ws_raw[32 * q : 32 * q + 4, :].bitcast(I32), w1_scales[0][4 * q : 4 * q + 4, :].bitcast(I32))
+            nc.scalar.dma_start(
+                xs_tab[32 * q + 4 : 32 * q + 8, :].bitcast(I32), x_scales[0][4 * q : 4 * q + 4, :].bitcast(I32)
+            )
+        for q in range(4):
+            nc.gpsimd.dma_start(ws_raw[32 * q : 32 * q + 4, :].bitcast(I32), w1_scales[0][4 * q : 4 * q + 4, :].bitcast(I32))
 
         warm_in = sb("warm_in", [P, 1], F32)
         warm_out = sb("warm_out", [P, 1], F32)
         nc.vector.memset(warm_in[:], 0.0)
         nc.scalar.activation(warm_out[:], warm_in[:], ACT.Exp)
 
-        ds_g = sb("ds_g", [P, S], U8)
+        ds_g = sb_at("ds_g", [P, S], U8, 768)
         ds_key = sb("ds_key", [P, S], U8)
         nc.vector.tensor_copy(ds_g[:], ds_tab[:].indirect(kidx_sb[:]))
         nc.vector.tensor_copy(
@@ -76,7 +80,9 @@ def tile_picked_softkeys_none_po_kernel(
         )
         for e in range(2):
             nc.scalar.dma_start(ds_key[2 + e : P : 32, :].bitcast(I32), ds_key[16 + e : P : 32, :].bitcast(I32))
-        d_g = sb("d_g", [P, S], U32)
+        w_raw = sb_at("w_raw", [P, 2 * S], U8, 0)
+        nc.sync.dma_start(w_raw[:].bitcast(I32), w1_words[0].bitcast(I32))
+        d_g = sb_at("d_g", [P, S], U32, 1024)
         d_key = sb("d_key", [P, S], U32)
         nc.vector.tensor_copy(d_g[:], d_tab[:].indirect(kidx_sb[:]))
         nc.vector.tensor_copy(
@@ -84,12 +90,12 @@ def tile_picked_softkeys_none_po_kernel(
             d_g[:].bitcast(I32).rearrange("p (c i t) -> p c t i", t=PACK, i=4),
         )
         xs_g = sb("xs_g", [P, S], U8)
-        x_g = sb("x_g", [P, S], U32)
+        x_g = sb_at("x_g", [P, S], U32, 12288)
         nc.vector.tensor_copy(xs_g[:], xs_tab[:].indirect(offs_sb[:]))
         nc.vector.tensor_copy(x_g[:], x_tab[:].indirect(offs_sb[:]))
 
-        w_key = sb("w_key", [P, 2 * S], U8)
-        ws_key = sb("ws_key", [P, S], U8)
+        w_key = sb_at("w_key", [P, 2 * S], U8, 4096)
+        ws_key = sb_at("ws_key", [P, S], U8, 4096 + 2 * S)
         nc.vector.tensor_copy(
             w_key[:].rearrange("p (t c i b) -> p c t i b", t=PACK, i=8, b=2),
             w_raw[:].rearrange("p (c i t b) -> p c t i b", t=PACK, i=8, b=2),
@@ -103,17 +109,23 @@ def tile_picked_softkeys_none_po_kernel(
         total = sb("total", [P, PACK], F32)
         neg = [sb("neg%d" % t, [P, S], F32) for t in range(PACK)]
         win = [sb("win%d" % t, [P, S], F32) for t in range(PACK)]
-        own = [sb("own%d" % t, [P, S], F32) for t in range(PACK)]
-        both = [sb("both%d" % t, [P, S], F32) for t in range(PACK)]
+        own = [[sb("own%d_%d" % (t, h), [P, HALF], F32) for h in range(2)] for t in range(PACK)]
+        both = [[sb("both%d_%d" % (t, h), [P, HALF], F32) for h in range(2)] for t in range(PACK)]
+
+        def own_exp(t, h):
+            nc.scalar.activation(
+                own[t][h][:], neg[t][:, HALF * h : HALF * (h + 1)], ACT.Exp, bias=low[:, t : t + 1], scale=-1.0
+            )
+
         for t in range(PACK):
             cols = slice(P * t, P * (t + 1))
-            score = psum.tile([P, S], F32, name="score%d" % t)
+            score = psum.tile([P, S], F32, name="score%d" % t, tag="bank%d" % t)
             nc.tensor.matmul_mx(
                 out=score[:],
                 lhsT=d_key[:, cols].bitcast(FP8X4),
                 lhsT_scale=ds_key[:, cols],
                 rhs=x_g[:].bitcast(FP8X4),
-                rhs_scale=xs_g[:],
+                rhs_scale=xs_g[4:P, :],
                 start=True,
                 stop=True,
             )
@@ -121,83 +133,107 @@ def tile_picked_softkeys_none_po_kernel(
             nc.scalar.activation(
                 win[t][:], neg[t][:], ACT.Exp, bias=low[:, t : t + 1], scale=-1.0, accum_out=total[:, t : t + 1]
             )
-            nc.scalar.activation(own[t][:], neg[t][:], ACT.Exp, bias=low[:, t : t + 1], scale=-1.0)
+            own_exp(t, 0)
 
         def join(t, h):
-            cols = slice(HALF * h, HALF * (h + 1))
             nc.vector.tensor_tensor(
-                both[t][:, cols], win[t][:].indirect(nb_sb[:, 16 * h : 16 * (h + 1)]), own[t][:, cols], ALU.add
+                both[t][h][:], win[t][:].indirect(nb_sb[:, 16 * h : 16 * (h + 1)]), own[t][h][:], ALU.add
             )
 
         inv = sb("inv", [P, PACK], F32)
         factor = sb("factor", [P, PACK], F32)
         z_rows = [sb("z_rows%d" % h, [P, PACK, HALF], BF16) for h in range(2)]
-        z_words = [sb("z_words%d" % h, [P, HALF * PACK], BF16) for h in range(2)]
-        z_codes = [sb("z_codes%d" % h, [P, HALF], U32) for h in range(2)]
-        z_scales = [sb("z_scales%d" % h, [P, HALF], U8) for h in range(2)]
+        z_words = [sb("z_words%d" % c, [P, CHUNK * PACK], BF16) for c in range(4)]
+        z_codes = [sb("z_codes%d" % c, [P, CHUNK], U32) for c in range(4)]
+        z_scales = [sb("z_scales%d" % c, [P, CHUNK], U8) for c in range(4)]
 
-        def weigh(h):
-            for t in range(PACK):
-                nc.scalar.activation(
-                    z_rows[h][:, t, :], both[t][:, HALF * h : HALF * (h + 1)], ACT.Copy, scale=factor[:, t : t + 1]
-                )
+        def weigh(t, h):
+            nc.scalar.activation(z_rows[h][:, t, :], both[t][h][:], ACT.Copy, scale=factor[:, t : t + 1])
 
-        def weave_z(h):
+        def weave_z(c):
+            h, o = divmod(CHUNK * c, HALF)
             nc.vector.tensor_copy(
-                z_words[h][:].rearrange("p (c i t) -> p c t i", t=PACK, i=4),
-                z_rows[h][:].rearrange("p t (c i) -> p c t i", i=4),
+                z_words[c][:].rearrange("p (c i t) -> p c t i", t=PACK, i=4),
+                z_rows[h][:, :, o : o + CHUNK].rearrange("p t (c i) -> p c t i", i=4),
             )
 
-        def quant_z(h):
-            nc.vector.quantize_mx(out=z_codes[h][:].bitcast(FP8X4), scales=z_scales[h][:], in_=z_words[h][:])
+        def quant_z(c):
+            nc.vector.quantize_mx(out=z_codes[c][:].bitcast(FP8X4), scales=z_scales[c][:], in_=z_words[c][:])
+
+        y_codes = sb("y_codes", [P, S], U32)
+        y_scales = sb("y_scales", [P, S], U8)
+        y = [sb("y%d" % c, [P, PACK, CHUNK], F32) for c in range(4)]
+        y_words = [sb("y_words%d" % c, [P, CHUNK * PACK], BF16) for c in range(4)]
+        out_rows = out_0.rearrange("(p t) n -> p t n", t=PACK)
+        out_codes = out_1[0].rearrange("p n t -> p (n t)").bitcast(I32)
+
+        def product(c):
+            for u in range(2):
+                acc = psum.tile([P, 2, CHUNK], F32, name="acc%d_%d" % (c, u), tag="bank%d" % ((4 + 2 * c + u) % 8))
+                for e in range(2):
+                    t = 2 * u + e
+                    nc.tensor.matmul_mx(
+                        out=acc[:, e, :],
+                        lhsT=w_key[:, 2 * P * t : 2 * P * (t + 1)].bitcast(FP4X4),
+                        lhsT_scale=ws_key[:, P * t : P * (t + 1)],
+                        rhs=z_codes[c][:].bitcast(FP8X4),
+                        rhs_scale=z_scales[c][:],
+                        start=True,
+                        stop=True,
+                    )
+                nc.scalar.copy(y[c][:, 2 * u : 2 * u + 2, :], acc[:])
+            nc.sync.dma_start(out_rows[:, :, CHUNK * c : CHUNK * (c + 1)], y[c][:])
+
+        def weave_y(c):
+            nc.vector.tensor_copy(
+                y_words[c][:].rearrange("p (c i t) -> p c t i", t=PACK, i=4),
+                y[c][:].rearrange("p t (c i) -> p c t i", i=4),
+            )
+
+        def quant_y(c):
+            cols = slice(CHUNK * c, CHUNK * (c + 1))
+            nc.vector.quantize_mx(out=y_codes[:, cols].bitcast(FP8X4), scales=y_scales[:, cols], in_=y_words[c][:])
+            if c % 2 == 1:
+                pair = slice(CHUNK * (c - 1), CHUNK * (c + 1))
+                nc.sync.dma_start(out_codes[:, pair], y_codes[:, pair].bitcast(I32))
 
         join(0, 0)
-        join(0, 1)
         join(1, 0)
-        join(1, 1)
         nc.vector.reciprocal(inv[:], total[:])
         join(2, 0)
         nc.vector.scalar_tensor_tensor(factor[:], inv[:], 32.0, gn_sb[:], ALU.mult, ALU.mult)
         join(3, 0)
-        weigh(0)
-        join(2, 1)
+        own_exp(0, 1)
+        own_exp(1, 1)
+        for t in range(PACK):
+            weigh(t, 0)
+        own_exp(2, 1)
+        own_exp(3, 1)
+        join(0, 1)
+        weigh(0, 1)
         weave_z(0)
-        join(3, 1)
-        quant_z(0)
-        weigh(1)
+        join(1, 1)
+        weigh(1, 1)
         weave_z(1)
+        quant_z(0)
+        join(2, 1)
+        weigh(2, 1)
         quant_z(1)
-
-        y_codes = sb("y_codes", [P, S], U32)
-        y_scales = sb("y_scales", [P, S], U8)
-        out_rows = out_0.rearrange("(p t) n -> p t n", t=PACK)
-        out_codes = out_1[0].rearrange("p n t -> p (n t)").bitcast(I32)
-        for c in range(S // CHUNK):
-            h, o = divmod(CHUNK * c, HALF)
-            cols = slice(CHUNK * c, CHUNK * (c + 1))
-            acc = psum.tile([P, PACK, CHUNK], F32, name="acc%d" % c)
-            for t in range(PACK):
-                nc.tensor.matmul_mx(
-                    out=acc[:, t, :],
-                    lhsT=w_key[:, 2 * P * t : 2 * P * (t + 1)].bitcast(FP4X4),
-                    lhsT_scale=ws_key[:, P * t : P * (t + 1)],
-                    rhs=z_codes[h][:, o : o + CHUNK].bitcast(FP8X4),
-                    rhs_scale=z_scales[h][:, o : o + CHUNK],
-                    start=True,
-                    stop=True,
-                )
-            y = sb("y%d" % c, [P, PACK, CHUNK], F32)
-            nc.scalar.copy(y[:], acc[:])
-            nc.sync.dma_start(out_rows[:, :, cols], y[:])
-            y_words = sb("y_words%d" % c, [P, CHUNK * PACK], BF16)
-            nc.vector.tensor_copy(
-                y_words[:].rearrange("p (c i t) -> p c t i", t=PACK, i=4),
-                y[:].rearrange("p t (c i) -> p c t i", i=4),
-            )
-            nc.vector.quantize_mx(out=y_codes[:, cols].bitcast(FP8X4), scales=y_scales[:, cols], in_=y_words[:])
-            if c % 2 == 1:
-                pair = slice(CHUNK * (c - 1), CHUNK * (c + 1))
-                nc.sync.dma_start(out_codes[:, pair], y_codes[:, pair].bitcast(I32))
+        join(3, 1)
+        product(0)
+        weigh(3, 1)
+        product(1)
+        weave_y(0)
+        weave_z(2)
+        weave_z(3)
+        quant_z(2)
+        quant_z(3)
+        product(2)
+        product(3)
+        quant_y(0)
+        for c in range(1, 4):
+            weave_y(c)
+            quant_y(c)
         for q in range(4):
             queue = nc.scalar if q % 2 == 0 else nc.sync
             queue.dma_start(out_2[0][4 * q : 4 * q + 4, :].bitcast(I32), y_scales[32 * q : 32 * q + 4, :].bitcast(I32))

@@ -42,30 +42,28 @@ def tile_picked_softkeys_none_po_kernel(
         nb_sb = sb("nb_sb", [P, S // 16], U16)
         d_tab = sb("d_tab", [P, TABLE], U32)
         x_tab = sb_at("x_tab", [P, TABLE], U32, 4096)
-        ds_tab = sb("ds_tab", [P, TABLE], U8)
+        ds_tab = sb_at("ds_tab", [P, TABLE], U8, 16384)
         xs_tab = sb_at("xs_tab", [P, TABLE], U8, 12288)
-        ws_raw = sb("ws_raw", [P, S], U8)
-        gn_sb = sb("gn_sb", [P, PACK], F32)
 
         nc.vector.memset(ds_tab[:].bitcast(I32), 0)
         nc.vector.memset(xs_tab[:].bitcast(I32), 0)
+        ws_raw = sb("ws_raw", [P, S], U8)
         nc.vector.memset(ws_raw[:].bitcast(I32), 0)
 
+        w_raw = sb("w_raw", [P, 2 * S], U8)
         nc.sync.dma_start(kidx_sb[:], kidx)
         nc.sync.dma_start(offs_sb[:], offs)
         nc.sync.dma_start(nb_sb[:], nb)
-        nc.sync.dma_start(gn_sb[:], gn.rearrange("(p t) o -> p (t o)", t=PACK))
         for e in range(2):
             nc.sync.dma_start(ds_tab[e:P:16, :].bitcast(I32), d_scales[0][e:16:2, :].bitcast(I32))
         nc.sync.dma_start(d_tab[:].bitcast(I32), d_words[0].rearrange("p n t -> p (n t)").bitcast(I32))
+        for a in range(4):
+            nc.sync.dma_start(xs_tab[4 + a : P : 32, :].bitcast(I32), x_scales[0][a:16:4, :].bitcast(I32))
         nc.sync.dma_start(x_tab[:].bitcast(I32), x_words[0].rearrange("p n t -> p (n t)").bitcast(I32))
-        for q in range(4):
-            nc.scalar.dma_start(
-                xs_tab[32 * q + 4 : 32 * q + 8, :].bitcast(I32), x_scales[0][4 * q : 4 * q + 4, :].bitcast(I32)
-            )
-        for q in range(4):
-            nc.gpsimd.dma_start(ws_raw[32 * q : 32 * q + 4, :].bitcast(I32), w1_scales[0][4 * q : 4 * q + 4, :].bitcast(I32))
 
+        nc.sync.dma_start(w_raw[:].bitcast(I32), w1_words[0].bitcast(I32))
+        for a in range(4):
+            nc.sync.dma_start(ws_raw[a:P:32, :].bitcast(I32), w1_scales[0][a:16:4, :].bitcast(I32))
         warm_in = sb("warm_in", [P, 1], F32)
         warm_out = sb("warm_out", [P, 1], F32)
         nc.vector.memset(warm_in[:], 0.0)
@@ -80,9 +78,7 @@ def tile_picked_softkeys_none_po_kernel(
         )
         for e in range(2):
             nc.scalar.dma_start(ds_key[2 + e : P : 32, :].bitcast(I32), ds_key[16 + e : P : 32, :].bitcast(I32))
-        w_raw = sb_at("w_raw", [P, 2 * S], U8, 0)
-        nc.sync.dma_start(w_raw[:].bitcast(I32), w1_words[0].bitcast(I32))
-        d_g = sb_at("d_g", [P, S], U32, 1024)
+        d_g = sb_at("d_g", [P, S], U32, 16384 + 512)
         d_key = sb("d_key", [P, S], U32)
         nc.vector.tensor_copy(d_g[:], d_tab[:].indirect(kidx_sb[:]))
         nc.vector.tensor_copy(
@@ -94,13 +90,15 @@ def tile_picked_softkeys_none_po_kernel(
         nc.vector.tensor_copy(xs_g[:], xs_tab[:].indirect(offs_sb[:]))
         nc.vector.tensor_copy(x_g[:], x_tab[:].indirect(offs_sb[:]))
 
+        gn_sb = sb_at("gn_sb", [P, PACK], F32, 4096 + 3 * S)
+        nc.sync.dma_start(gn_sb[:], gn.rearrange("(p t) o -> p (t o)", t=PACK))
         w_key = sb_at("w_key", [P, 2 * S], U8, 4096)
         ws_key = sb_at("ws_key", [P, S], U8, 4096 + 2 * S)
         nc.vector.tensor_copy(
             w_key[:].rearrange("p (t c i b) -> p c t i b", t=PACK, i=8, b=2),
             w_raw[:].rearrange("p (c i t b) -> p c t i b", t=PACK, i=8, b=2),
         )
-        nc.vector.tensor_copy(
+        nc.gpsimd.tensor_copy(
             ws_key[:].rearrange("p (t c i) -> p c t i", t=PACK, i=16),
             ws_raw[:].rearrange("p (c i t) -> p c t i", t=PACK, i=16),
         )
@@ -109,8 +107,13 @@ def tile_picked_softkeys_none_po_kernel(
         total = sb("total", [P, PACK], F32)
         neg = [sb("neg%d" % t, [P, S], F32) for t in range(PACK)]
         win = [sb("win%d" % t, [P, S], F32) for t in range(PACK)]
-        own = [[sb("own%d_%d" % (t, h), [P, HALF], F32) for h in range(2)] for t in range(PACK)]
-        both = [[sb("both%d_%d" % (t, h), [P, HALF], F32) for h in range(2)] for t in range(PACK)]
+        held = {}
+
+        def sb_or_held(name, shape, dtype):
+            return sb_at(name, shape, dtype, held[name]) if name in held else sb(name, shape, dtype)
+
+        own = [[sb_or_held("own%d_%d" % (t, h), [P, HALF], F32) for h in range(2)] for t in range(PACK)]
+        both = [[sb_or_held("both%d_%d" % (t, h), [P, HALF], F32) for h in range(2)] for t in range(PACK)]
 
         def own_exp(t, h):
             nc.scalar.activation(
@@ -140,10 +143,10 @@ def tile_picked_softkeys_none_po_kernel(
                 both[t][h][:], win[t][:].indirect(nb_sb[:, 16 * h : 16 * (h + 1)]), own[t][h][:], ALU.add
             )
 
-        inv = sb("inv", [P, PACK], F32)
+        inv = sb_or_held("inv", [P, PACK], F32)
         factor = sb("factor", [P, PACK], F32)
-        z_rows = [sb("z_rows%d" % h, [P, PACK, HALF], BF16) for h in range(2)]
-        z_words = [sb("z_words%d" % c, [P, CHUNK * PACK], BF16) for c in range(4)]
+        z_rows = [sb_or_held("z_rows%d" % h, [P, PACK, HALF], BF16) for h in range(2)]
+        z_words = [sb_or_held("z_words%d" % c, [P, CHUNK * PACK], BF16) for c in range(4)]
         z_codes = [sb("z_codes%d" % c, [P, CHUNK], U32) for c in range(4)]
         z_scales = [sb("z_scales%d" % c, [P, CHUNK], U8) for c in range(4)]
 
@@ -152,7 +155,8 @@ def tile_picked_softkeys_none_po_kernel(
 
         def weave_z(c):
             h, o = divmod(CHUNK * c, HALF)
-            nc.vector.tensor_copy(
+            copy = nc.scalar.copy if c < 0 else nc.vector.tensor_copy
+            copy(
                 z_words[c][:].rearrange("p (c i t) -> p c t i", t=PACK, i=4),
                 z_rows[h][:, :, o : o + CHUNK].rearrange("p t (c i) -> p c t i", i=4),
             )
@@ -193,8 +197,8 @@ def tile_picked_softkeys_none_po_kernel(
         def quant_y(c):
             cols = slice(CHUNK * c, CHUNK * (c + 1))
             nc.vector.quantize_mx(out=y_codes[:, cols].bitcast(FP8X4), scales=y_scales[:, cols], in_=y_words[c][:])
-            if c % 2 == 1:
-                pair = slice(CHUNK * (c - 1), CHUNK * (c + 1))
+            if c >= 2:
+                pair = slice(0 if c == 2 else CHUNK * c, CHUNK * (c + 1))
                 nc.sync.dma_start(out_codes[:, pair], y_codes[:, pair].bitcast(I32))
 
         join(0, 0)

@@ -42,56 +42,55 @@ def tile_picked_softkeys_none_po_kernel(
         nb_sb = sb("nb_sb", [P, S // 16], U16)
         d_tab = sb("d_tab", [P, TABLE], U32)
         x_tab = sb_at("x_tab", [P, TABLE], U32, 4096)
-        ds_tab = sb_at("ds_tab", [P, TABLE], U8, 16384)
-        xs_tab = sb_at("xs_tab", [P, TABLE], U8, 12288)
+        ds_tab = sb("ds_tab", [P, TABLE], U8)
+        xs_tab = sb("xs_tab", [P, TABLE], U8)
 
         nc.vector.memset(ds_tab[:].bitcast(I32), 0)
-        nc.vector.memset(xs_tab[:].bitcast(I32), 0)
-        ws_raw = sb("ws_raw", [P, S], U8)
-        nc.vector.memset(ws_raw[:].bitcast(I32), 0)
+        nc.gpsimd.memset(xs_tab[:].bitcast(I32), 0)
 
         w_raw = sb("w_raw", [P, 2 * S], U8)
+        gn_sb = sb("gn_sb", [P, PACK], F32)
+        gn32 = sb("gn32", [P, PACK], F32)
         nc.sync.dma_start(kidx_sb[:], kidx)
         nc.sync.dma_start(offs_sb[:], offs)
-        nc.sync.dma_start(nb_sb[:], nb)
         for e in range(2):
             nc.sync.dma_start(ds_tab[e:P:16, :].bitcast(I32), d_scales[0][e:16:2, :].bitcast(I32))
+        for e in range(2):
+            nc.sync.dma_start(xs_tab[e:P:16, :].bitcast(I32), x_scales[0][e:16:2, :].bitcast(I32))
         nc.sync.dma_start(d_tab[:].bitcast(I32), d_words[0].rearrange("p n t -> p (n t)").bitcast(I32))
-        for a in range(4):
-            nc.sync.dma_start(xs_tab[4 + a : P : 32, :].bitcast(I32), x_scales[0][a:16:4, :].bitcast(I32))
         nc.sync.dma_start(x_tab[:].bitcast(I32), x_words[0].rearrange("p n t -> p (n t)").bitcast(I32))
-
         nc.sync.dma_start(w_raw[:].bitcast(I32), w1_words[0].bitcast(I32))
-        for a in range(4):
-            nc.sync.dma_start(ws_raw[a:P:32, :].bitcast(I32), w1_scales[0][a:16:4, :].bitcast(I32))
-        warm_in = sb("warm_in", [P, 1], F32)
-        warm_out = sb("warm_out", [P, 1], F32)
-        nc.vector.memset(warm_in[:], 0.0)
-        nc.scalar.activation(warm_out[:], warm_in[:], ACT.Exp)
+        nc.sync.dma_start(nb_sb[:], nb)
+        nc.scalar.dma_start(gn_sb[:], gn.rearrange("(p t) o -> p (t o)", t=PACK))
+        nc.scalar.activation(gn32[:], gn_sb[:], ACT.Copy, scale=32.0)
 
-        ds_g = sb_at("ds_g", [P, S], U8, 768)
-        ds_key = sb("ds_key", [P, S], U8)
+        ds_g = sb("ds_g", [P, S], U8)
+        xs_g = sb_at("xs_g", [P, S], U8, 0)
+        planes = sb("planes", [P, 2 * S], U8)
+        ds_key = planes[:, 0:S]
         nc.vector.tensor_copy(ds_g[:], ds_tab[:].indirect(kidx_sb[:]))
+        nc.vector.tensor_copy(xs_g[:], xs_tab[:].indirect(offs_sb[:]))
         nc.vector.tensor_copy(
-            ds_key[:].rearrange("p (t c i) -> p c t i", t=PACK, i=16),
+            ds_key.rearrange("p (t c i) -> p c t i", t=PACK, i=16),
             ds_g[:].rearrange("p (c i t) -> p c t i", t=PACK, i=16),
         )
+        nc.vector.tensor_copy(planes[:, S : 2 * S].bitcast(I32), xs_g[:].bitcast(I32))
         for e in range(2):
-            nc.scalar.dma_start(ds_key[2 + e : P : 32, :].bitcast(I32), ds_key[16 + e : P : 32, :].bitcast(I32))
-        d_g = sb_at("d_g", [P, S], U32, 16384 + 512)
+            nc.scalar.dma_start(planes[2 + e : P : 32, :].bitcast(I32), planes[16 + e : P : 32, :].bitcast(I32))
+        ws_raw = sb_at("ws_raw", [P, S], U8, 0)
+        nc.gpsimd.memset(ws_raw[:].bitcast(I32), 0)
+        for a in range(4):
+            nc.sync.dma_start(ws_raw[a:P:32, :].bitcast(I32), w1_scales[0][a:16:4, :].bitcast(I32))
+        d_g = sb("d_g", [P, S], U32)
         d_key = sb("d_key", [P, S], U32)
         nc.vector.tensor_copy(d_g[:], d_tab[:].indirect(kidx_sb[:]))
         nc.vector.tensor_copy(
             d_key[:].bitcast(I32).rearrange("p (t c i) -> p c t i", t=PACK, i=4),
             d_g[:].bitcast(I32).rearrange("p (c i t) -> p c t i", t=PACK, i=4),
         )
-        xs_g = sb("xs_g", [P, S], U8)
-        x_g = sb_at("x_g", [P, S], U32, 12288)
-        nc.vector.tensor_copy(xs_g[:], xs_tab[:].indirect(offs_sb[:]))
+        x_g = sb("x_g", [P, S], U32)
         nc.vector.tensor_copy(x_g[:], x_tab[:].indirect(offs_sb[:]))
 
-        gn_sb = sb_at("gn_sb", [P, PACK], F32, 4096 + 3 * S)
-        nc.sync.dma_start(gn_sb[:], gn.rearrange("(p t) o -> p (t o)", t=PACK))
         w_key = sb_at("w_key", [P, 2 * S], U8, 4096)
         ws_key = sb_at("ws_key", [P, S], U8, 4096 + 2 * S)
         nc.vector.tensor_copy(
@@ -126,9 +125,9 @@ def tile_picked_softkeys_none_po_kernel(
             nc.tensor.matmul_mx(
                 out=score[:],
                 lhsT=d_key[:, cols].bitcast(FP8X4),
-                lhsT_scale=ds_key[:, cols],
+                lhsT_scale=planes[:, cols],
                 rhs=x_g[:].bitcast(FP8X4),
-                rhs_scale=xs_g[4:P, :],
+                rhs_scale=planes[:, S : 2 * S],
                 start=True,
                 stop=True,
             )
@@ -205,7 +204,7 @@ def tile_picked_softkeys_none_po_kernel(
         join(1, 0)
         nc.vector.reciprocal(inv[:], total[:])
         join(2, 0)
-        nc.vector.scalar_tensor_tensor(factor[:], inv[:], 32.0, gn_sb[:], ALU.mult, ALU.mult)
+        nc.vector.tensor_tensor(factor[:], inv[:], gn32[:], ALU.mult)
         join(3, 0)
         own_exp(0, 1)
         own_exp(1, 1)

@@ -46,25 +46,21 @@ def tile_picked_softkeys_none_po_kernel(
         xs_tab = sb("xs_tab", [P, TABLE], U8)
 
         nc.vector.memset(ds_tab[:].bitcast(I32), 0)
-        nc.gpsimd.memset(xs_tab[:].bitcast(I32), 0)
+        nc.vector.memset(xs_tab[:].bitcast(I32), 0)
 
-        w_raw = sb("w_raw", [P, 2 * S], U8)
         gn_sb = sb("gn_sb", [P, PACK], F32)
         gn32 = sb("gn32", [P, PACK], F32)
         nc.sync.dma_start(kidx_sb[:], kidx)
         nc.sync.dma_start(offs_sb[:], offs)
-        for e in range(2):
-            nc.sync.dma_start(ds_tab[e:P:16, :].bitcast(I32), d_scales[0][e:16:2, :].bitcast(I32))
-        for e in range(2):
-            nc.sync.dma_start(xs_tab[e:P:16, :].bitcast(I32), x_scales[0][e:16:2, :].bitcast(I32))
+        nc.sync.dma_start(ds_tab[0:P:8, :].bitcast(I32), d_scales[0].bitcast(I32))
+        nc.sync.dma_start(xs_tab[0:P:8, :].bitcast(I32), x_scales[0].bitcast(I32))
         nc.sync.dma_start(d_tab[:].bitcast(I32), d_words[0].rearrange("p n t -> p (n t)").bitcast(I32))
         nc.sync.dma_start(x_tab[:].bitcast(I32), x_words[0].rearrange("p n t -> p (n t)").bitcast(I32))
-        nc.sync.dma_start(w_raw[:].bitcast(I32), w1_words[0].bitcast(I32))
         nc.sync.dma_start(nb_sb[:], nb)
         nc.scalar.dma_start(gn_sb[:], gn.rearrange("(p t) o -> p (t o)", t=PACK))
         nc.scalar.activation(gn32[:], gn_sb[:], ACT.Copy, scale=32.0)
 
-        ds_g = sb("ds_g", [P, S], U8)
+        ds_g = sb_at("ds_g", [P, S], U8, 1024)
         xs_g = sb_at("xs_g", [P, S], U8, 0)
         planes = sb("planes", [P, 2 * S], U8)
         ds_key = planes[:, 0:S]
@@ -75,10 +71,12 @@ def tile_picked_softkeys_none_po_kernel(
             ds_g[:].rearrange("p (c i t) -> p c t i", t=PACK, i=16),
         )
         nc.vector.tensor_copy(planes[:, S : 2 * S].bitcast(I32), xs_g[:].bitcast(I32))
-        for e in range(2):
-            nc.scalar.dma_start(planes[2 + e : P : 32, :].bitcast(I32), planes[16 + e : P : 32, :].bitcast(I32))
-        ws_raw = sb_at("ws_raw", [P, S], U8, 0)
-        nc.gpsimd.memset(ws_raw[:].bitcast(I32), 0)
+        for j in range(1, 4):
+            nc.scalar.dma_start(planes[j:P:32, :].bitcast(I32), planes[8 * j : P : 32, :].bitcast(I32))
+        w_raw = sb_at("w_raw", [P, 2 * S], U8, 0)
+        nc.sync.dma_start(w_raw[:].bitcast(I32), w1_words[0].bitcast(I32))
+        ws_raw = sb_at("ws_raw", [P, S], U8, 1024)
+        nc.vector.memset(ws_raw[:].bitcast(I32), 0)
         for a in range(4):
             nc.sync.dma_start(ws_raw[a:P:32, :].bitcast(I32), w1_scales[0][a:16:4, :].bitcast(I32))
         d_g = sb("d_g", [P, S], U32)
@@ -88,8 +86,9 @@ def tile_picked_softkeys_none_po_kernel(
             d_key[:].bitcast(I32).rearrange("p (t c i) -> p c t i", t=PACK, i=4),
             d_g[:].bitcast(I32).rearrange("p (c i t) -> p c t i", t=PACK, i=4),
         )
-        x_g = sb("x_g", [P, S], U32)
-        nc.vector.tensor_copy(x_g[:], x_tab[:].indirect(offs_sb[:]))
+        x_g = [sb("x_g%d" % h, [P, HALF], U32) for h in range(2)]
+        for h in range(2):
+            nc.vector.tensor_copy(x_g[h][:], x_tab[:].indirect(offs_sb[:, 16 * h : 16 * (h + 1)]))
 
         w_key = sb_at("w_key", [P, 2 * S], U8, 4096)
         ws_key = sb_at("ws_key", [P, S], U8, 4096 + 2 * S)
@@ -97,72 +96,23 @@ def tile_picked_softkeys_none_po_kernel(
             w_key[:].rearrange("p (t c i b) -> p c t i b", t=PACK, i=8, b=2),
             w_raw[:].rearrange("p (c i t b) -> p c t i b", t=PACK, i=8, b=2),
         )
-        nc.gpsimd.tensor_copy(
+        nc.vector.tensor_copy(
             ws_key[:].rearrange("p (t c i) -> p c t i", t=PACK, i=16),
             ws_raw[:].rearrange("p (c i t) -> p c t i", t=PACK, i=16),
         )
 
         low = sb("low", [P, PACK], F32)
         total = sb("total", [P, PACK], F32)
+        inv = sb("inv", [P, PACK], F32)
+        factor = sb("factor", [P, PACK], F32)
         neg = [sb("neg%d" % t, [P, S], F32) for t in range(PACK)]
         win = [sb("win%d" % t, [P, S], F32) for t in range(PACK)]
-        held = {}
-
-        def sb_or_held(name, shape, dtype):
-            return sb_at(name, shape, dtype, held[name]) if name in held else sb(name, shape, dtype)
-
-        own = [[sb_or_held("own%d_%d" % (t, h), [P, HALF], F32) for h in range(2)] for t in range(PACK)]
-        both = [[sb_or_held("both%d_%d" % (t, h), [P, HALF], F32) for h in range(2)] for t in range(PACK)]
-
-        def own_exp(t, h):
-            nc.scalar.activation(
-                own[t][h][:], neg[t][:, HALF * h : HALF * (h + 1)], ACT.Exp, bias=low[:, t : t + 1], scale=-1.0
-            )
-
-        for t in range(PACK):
-            cols = slice(P * t, P * (t + 1))
-            score = psum.tile([P, S], F32, name="score%d" % t, tag="bank%d" % t)
-            nc.tensor.matmul_mx(
-                out=score[:],
-                lhsT=d_key[:, cols].bitcast(FP8X4),
-                lhsT_scale=planes[:, cols],
-                rhs=x_g[:].bitcast(FP8X4),
-                rhs_scale=planes[:, S : 2 * S],
-                start=True,
-                stop=True,
-            )
-            nc.vector.tensor_scalar(neg[t][:], score[:], -0.03125, None, ALU.mult, ALU.min, accum_out=low[:, t : t + 1])
-            nc.scalar.activation(
-                win[t][:], neg[t][:], ACT.Exp, bias=low[:, t : t + 1], scale=-1.0, accum_out=total[:, t : t + 1]
-            )
-            own_exp(t, 0)
-
-        def join(t, h):
-            nc.vector.tensor_tensor(
-                both[t][h][:], win[t][:].indirect(nb_sb[:, 16 * h : 16 * (h + 1)]), own[t][h][:], ALU.add
-            )
-
-        inv = sb_or_held("inv", [P, PACK], F32)
-        factor = sb("factor", [P, PACK], F32)
-        z_rows = [sb_or_held("z_rows%d" % h, [P, PACK, HALF], BF16) for h in range(2)]
-        z_words = [sb_or_held("z_words%d" % c, [P, CHUNK * PACK], BF16) for c in range(4)]
+        plain = {}
+        both = {}
+        z_rows = {}
+        z_words = [sb("z_words%d" % c, [P, CHUNK * PACK], BF16) for c in range(4)]
         z_codes = [sb("z_codes%d" % c, [P, CHUNK], U32) for c in range(4)]
         z_scales = [sb("z_scales%d" % c, [P, CHUNK], U8) for c in range(4)]
-
-        def weigh(t, h):
-            nc.scalar.activation(z_rows[h][:, t, :], both[t][h][:], ACT.Copy, scale=factor[:, t : t + 1])
-
-        def weave_z(c):
-            h, o = divmod(CHUNK * c, HALF)
-            copy = nc.scalar.copy if c < 0 else nc.vector.tensor_copy
-            copy(
-                z_words[c][:].rearrange("p (c i t) -> p c t i", t=PACK, i=4),
-                z_rows[h][:, :, o : o + CHUNK].rearrange("p t (c i) -> p c t i", i=4),
-            )
-
-        def quant_z(c):
-            nc.vector.quantize_mx(out=z_codes[c][:].bitcast(FP8X4), scales=z_scales[c][:], in_=z_words[c][:])
-
         y_codes = sb("y_codes", [P, S], U32)
         y_scales = sb("y_scales", [P, S], U8)
         y = [sb("y%d" % c, [P, PACK, CHUNK], F32) for c in range(4)]
@@ -170,27 +120,87 @@ def tile_picked_softkeys_none_po_kernel(
         out_rows = out_0.rearrange("(p t) n -> p t n", t=PACK)
         out_codes = out_1[0].rearrange("p n t -> p (n t)").bitcast(I32)
 
-        def product(c):
-            for u in range(2):
-                acc = psum.tile([P, 2, CHUNK], F32, name="acc%d_%d" % (c, u), tag="bank%d" % ((4 + 2 * c + u) % 8))
-                for e in range(2):
-                    t = 2 * u + e
-                    nc.tensor.matmul_mx(
-                        out=acc[:, e, :],
-                        lhsT=w_key[:, 2 * P * t : 2 * P * (t + 1)].bitcast(FP4X4),
-                        lhsT_scale=ws_key[:, P * t : P * (t + 1)],
-                        rhs=z_codes[c][:].bitcast(FP8X4),
-                        rhs_scale=z_scales[c][:],
-                        start=True,
-                        stop=True,
-                    )
-                nc.scalar.copy(y[c][:, 2 * u : 2 * u + 2, :], acc[:])
+        def own_exp(t, c, n):
+            tile = sb("own%d_%d" % (t, c), [P, CHUNK * n], F32)
+            nc.scalar.activation(
+                tile[:], neg[t][:, CHUNK * c : CHUNK * (c + n)], ACT.Exp, bias=low[:, t : t + 1], scale=-1.0
+            )
+            for e in range(n):
+                plain[t, c + e] = (tile, e)
+
+        def scores(t):
+            cols = slice(P * t, P * (t + 1))
+            score = psum.tile([P, S], F32, name="score%d" % t, tag="bank%d" % t)
+            for h in range(2):
+                nc.tensor.matmul_mx(
+                    out=score[:, HALF * h : HALF * (h + 1)],
+                    lhsT=d_key[:, cols].bitcast(FP8X4),
+                    lhsT_scale=planes[:, cols],
+                    rhs=x_g[h][:].bitcast(FP8X4),
+                    rhs_scale=planes[:, S + HALF * h : S + HALF * (h + 1)],
+                    start=True,
+                    stop=True,
+                )
+            nc.vector.tensor_scalar(neg[t][:], score[:], -0.03125, None, ALU.mult, ALU.min, accum_out=low[:, t : t + 1])
+            nc.scalar.activation(
+                win[t][:], neg[t][:], ACT.Exp, bias=low[:, t : t + 1], scale=-1.0, accum_out=total[:, t : t + 1]
+            )
+
+        def join(t, c, n):
+            tile = sb("both%d_%d" % (t, c), [P, CHUNK * n], F32)
+            own, o = plain[t, c]
+            nc.vector.tensor_tensor(
+                tile[:], win[t][:].indirect(nb_sb[:, 8 * c : 8 * (c + n)]), own[:, CHUNK * o : CHUNK * (o + n)], ALU.add
+            )
+            for e in range(n):
+                both[t, c + e] = (tile, e)
+
+        def weigh(t, c, n):
+            if t == 0:
+                rows = sb("z_rows%d" % c, [P, PACK, CHUNK * n], BF16)
+                for e in range(n):
+                    z_rows[c + e] = (rows, e)
+            rows, r = z_rows[c]
+            tile, o = both[t, c]
+            nc.scalar.activation(
+                rows[:, t, CHUNK * r : CHUNK * (r + n)],
+                tile[:, CHUNK * o : CHUNK * (o + n)],
+                ACT.Copy,
+                scale=factor[:, t : t + 1],
+            )
+
+        def weave_z(c):
+            rows, r = z_rows[c]
+            nc.vector.tensor_copy(
+                z_words[c][:].rearrange("p (c i t) -> p c t i", t=PACK, i=4),
+                rows[:, :, CHUNK * r : CHUNK * (r + 1)].rearrange("p t (c i) -> p c t i", i=4),
+            )
+
+        def quant_z(c):
+            nc.vector.quantize_mx(out=z_codes[c][:].bitcast(FP8X4), scales=z_scales[c][:], in_=z_words[c][:])
+
+        def product(c, bank):
+            acc = psum.tile([P, PACK, CHUNK], F32, name="acc%d" % bank, tag="bank%d" % bank)
+            for t in range(PACK):
+                nc.tensor.matmul_mx(
+                    out=acc[:, t, :],
+                    lhsT=w_key[:, 2 * P * t : 2 * P * (t + 1)].bitcast(FP4X4),
+                    lhsT_scale=ws_key[:, P * t : P * (t + 1)],
+                    rhs=z_codes[c][:].bitcast(FP8X4),
+                    rhs_scale=z_scales[c][:],
+                    start=True,
+                    stop=True,
+                )
+            return acc
+
+        def empty(c, acc):
+            nc.scalar.copy(y[c][:], acc[:])
             nc.sync.dma_start(out_rows[:, :, CHUNK * c : CHUNK * (c + 1)], y[c][:])
 
-        def weave_y(c):
-            nc.vector.tensor_copy(
+        def weave_y(c, copy, source):
+            copy(
                 y_words[c][:].rearrange("p (c i t) -> p c t i", t=PACK, i=4),
-                y[c][:].rearrange("p t (c i) -> p c t i", i=4),
+                source[:].rearrange("p t (c i) -> p c t i", i=4),
             )
 
         def quant_y(c):
@@ -200,43 +210,69 @@ def tile_picked_softkeys_none_po_kernel(
                 pair = slice(0 if c == 2 else CHUNK * c, CHUNK * (c + 1))
                 nc.sync.dma_start(out_codes[:, pair], y_codes[:, pair].bitcast(I32))
 
-        join(0, 0)
-        join(1, 0)
+        scores(0)
+        own_exp(0, 0, 2)
+        scores(1)
+        own_exp(1, 0, 2)
+        scores(2)
+        own_exp(2, 0, 2)
+        scores(3)
+        own_exp(3, 0, 2)
+        join(0, 0, 2)
+        join(1, 0, 2)
+        join(2, 0, 2)
         nc.vector.reciprocal(inv[:], total[:])
-        join(2, 0)
+        join(3, 0, 2)
         nc.vector.tensor_tensor(factor[:], inv[:], gn32[:], ALU.mult)
-        join(3, 0)
-        own_exp(0, 1)
-        own_exp(1, 1)
-        for t in range(PACK):
-            weigh(t, 0)
-        own_exp(2, 1)
-        own_exp(3, 1)
-        join(0, 1)
-        weigh(0, 1)
+        own_exp(0, 2, 2)
+        own_exp(1, 2, 2)
+        weigh(0, 0, 2)
+        weigh(1, 0, 2)
+        weigh(2, 0, 2)
+        weigh(3, 0, 2)
+        own_exp(2, 2, 2)
+        own_exp(3, 2, 2)
+        join(0, 2, 1)
+        join(1, 2, 1)
+        join(0, 3, 1)
         weave_z(0)
-        join(1, 1)
-        weigh(1, 1)
+        join(2, 2, 1)
         weave_z(1)
         quant_z(0)
-        join(2, 1)
-        weigh(2, 1)
+        acc0 = product(0, 4)
+        join(3, 2, 1)
         quant_z(1)
-        join(3, 1)
-        product(0)
-        weigh(3, 1)
-        product(1)
-        weave_y(0)
+        acc1 = product(1, 5)
+        weigh(0, 2, 1)
+        weigh(1, 2, 1)
+        weigh(2, 2, 1)
+        weigh(3, 2, 1)
+        join(1, 3, 1)
+        join(2, 3, 1)
         weave_z(2)
-        weave_z(3)
+        join(3, 3, 1)
         quant_z(2)
-        quant_z(3)
-        product(2)
-        product(3)
+        acc2 = product(2, 6)
+        weigh(0, 3, 1)
+        weigh(1, 3, 1)
+        weigh(2, 3, 1)
+        weigh(3, 3, 1)
+        empty(0, acc0)
+        empty(1, acc1)
+        weave_y(0, nc.vector.tensor_copy, y[0])
+        weave_z(3)
         quant_y(0)
-        for c in range(1, 4):
-            weave_y(c)
-            quant_y(c)
+        quant_z(3)
+        twin3 = product(3, 0)
+        acc3 = product(3, 7)
+        empty(2, acc2)
+        weave_y(1, nc.vector.tensor_copy, y[1])
+        weave_y(2, nc.vector.tensor_copy, y[2])
+        quant_y(1)
+        quant_y(2)
+        weave_y(3, nc.vector.tensor_copy, twin3)
+        empty(3, acc3)
+        quant_y(3)
         for q in range(4):
             queue = nc.scalar if q % 2 == 0 else nc.sync
             queue.dma_start(out_2[0][4 * q : 4 * q + 4, :].bitcast(I32), y_scales[32 * q : 32 * q + 4, :].bitcast(I32))

@@ -42,13 +42,12 @@ def tile_picked_softkeys_none_po_kernel(
         nb_sb = sb("nb_sb", [P, S // 16], U16)
         d_tab = sb("d_tab", [P, TABLE], U32)
         x_tab = sb_at("x_tab", [P, TABLE], U32, 4096)
-        ds_tab = sb("ds_tab", [P, TABLE], U8)
+        ds_tab = sb_at("ds_tab", [P, TABLE], U8, 16384)
         xs_tab = sb("xs_tab", [P, TABLE], U8)
 
         nc.vector.memset(ds_tab[:].bitcast(I32), 0)
         nc.vector.memset(xs_tab[:].bitcast(I32), 0)
 
-        gn_sb = sb("gn_sb", [P, PACK], F32)
         gn32 = sb("gn32", [P, PACK], F32)
         nc.sync.dma_start(kidx_sb[:], kidx)
         nc.sync.dma_start(offs_sb[:], offs)
@@ -57,14 +56,15 @@ def tile_picked_softkeys_none_po_kernel(
         nc.sync.dma_start(d_tab[:].bitcast(I32), d_words[0].rearrange("p n t -> p (n t)").bitcast(I32))
         nc.sync.dma_start(x_tab[:].bitcast(I32), x_words[0].rearrange("p n t -> p (n t)").bitcast(I32))
         nc.sync.dma_start(nb_sb[:], nb)
-        nc.scalar.dma_start(gn_sb[:], gn.rearrange("(p t) o -> p (t o)", t=PACK))
-        nc.scalar.activation(gn32[:], gn_sb[:], ACT.Copy, scale=32.0)
 
         ds_g = sb_at("ds_g", [P, S], U8, 1024)
         xs_g = sb_at("xs_g", [P, S], U8, 0)
         planes = sb("planes", [P, 2 * S], U8)
         ds_key = planes[:, 0:S]
         nc.vector.tensor_copy(ds_g[:], ds_tab[:].indirect(kidx_sb[:]))
+        gn_sb = sb_at("gn_sb", [P, PACK], F32, 16384)
+        nc.scalar.dma_start(gn_sb[:], gn.rearrange("(p t) o -> p (t o)", t=PACK))
+        nc.scalar.activation(gn32[:], gn_sb[:], ACT.Copy, scale=32.0)
         nc.vector.tensor_copy(xs_g[:], xs_tab[:].indirect(offs_sb[:]))
         nc.vector.tensor_copy(
             ds_key.rearrange("p (t c i) -> p c t i", t=PACK, i=16),
@@ -80,7 +80,7 @@ def tile_picked_softkeys_none_po_kernel(
         for a in range(4):
             nc.sync.dma_start(ws_raw[a:P:32, :].bitcast(I32), w1_scales[0][a:16:4, :].bitcast(I32))
         d_g = sb("d_g", [P, S], U32)
-        d_key = sb("d_key", [P, S], U32)
+        d_key = sb_at("d_key", [P, S], U32, 2048)
         nc.vector.tensor_copy(d_g[:], d_tab[:].indirect(kidx_sb[:]))
         nc.vector.tensor_copy(
             d_key[:].bitcast(I32).rearrange("p (t c i) -> p c t i", t=PACK, i=4),
@@ -90,16 +90,21 @@ def tile_picked_softkeys_none_po_kernel(
         for h in range(2):
             nc.vector.tensor_copy(x_g[h][:], x_tab[:].indirect(offs_sb[:, 16 * h : 16 * (h + 1)]))
 
-        w_key = sb_at("w_key", [P, 2 * S], U8, 4096)
-        ws_key = sb_at("ws_key", [P, S], U8, 4096 + 2 * S)
-        nc.vector.tensor_copy(
-            w_key[:].rearrange("p (t c i b) -> p c t i b", t=PACK, i=8, b=2),
-            w_raw[:].rearrange("p (c i t b) -> p c t i b", t=PACK, i=8, b=2),
-        )
-        nc.vector.tensor_copy(
-            ws_key[:].rearrange("p (t c i) -> p c t i", t=PACK, i=16),
-            ws_raw[:].rearrange("p (c i t) -> p c t i", t=PACK, i=16),
-        )
+        keys = {}
+
+        def deal_w():
+            keys["w"] = sb_at("w_key", [P, 2 * S], U8, 4096)
+            nc.gpsimd.tensor_copy(
+                keys["w"][:].rearrange("p (t c i b) -> p c t i b", t=PACK, i=8, b=2),
+                w_raw[:].rearrange("p (c i t b) -> p c t i b", t=PACK, i=8, b=2),
+            )
+
+        def deal_ws():
+            keys["ws"] = sb_at("ws_key", [P, S], U8, 4096 + 2 * S)
+            nc.gpsimd.tensor_copy(
+                keys["ws"][:].rearrange("p (t c i) -> p c t i", t=PACK, i=16),
+                ws_raw[:].rearrange("p (c i t) -> p c t i", t=PACK, i=16),
+            )
 
         low = sb("low", [P, PACK], F32)
         total = sb("total", [P, PACK], F32)
@@ -110,13 +115,13 @@ def tile_picked_softkeys_none_po_kernel(
         plain = {}
         both = {}
         z_rows = {}
-        z_words = [sb("z_words%d" % c, [P, CHUNK * PACK], BF16) for c in range(4)]
-        z_codes = [sb("z_codes%d" % c, [P, CHUNK], U32) for c in range(4)]
-        z_scales = [sb("z_scales%d" % c, [P, CHUNK], U8) for c in range(4)]
+        z_words = {}
+        z_quant = {}
+        y = {}
+        y_words = {}
+        y_pair = sb("y_pair", [P, HALF * PACK], BF16)
         y_codes = sb("y_codes", [P, S], U32)
         y_scales = sb("y_scales", [P, S], U8)
-        y = [sb("y%d" % c, [P, PACK, CHUNK], F32) for c in range(4)]
-        y_words = [sb("y_words%d" % c, [P, CHUNK * PACK], BF16) for c in range(4)]
         out_rows = out_0.rearrange("(p t) n -> p t n", t=PACK)
         out_codes = out_1[0].rearrange("p n t -> p (n t)").bitcast(I32)
 
@@ -128,23 +133,46 @@ def tile_picked_softkeys_none_po_kernel(
             for e in range(n):
                 plain[t, c + e] = (tile, e)
 
-        def scores(t):
+        first = sb("first", [P, PACK], F32)
+
+        def score_pass(out, t, h):
             cols = slice(P * t, P * (t + 1))
+            nc.tensor.matmul_mx(
+                out=out,
+                lhsT=d_key[:, cols].bitcast(FP8X4),
+                lhsT_scale=planes[:, cols],
+                rhs=x_g[h][:].bitcast(FP8X4),
+                rhs_scale=planes[:, S + HALF * h : S + HALF * (h + 1)],
+                start=True,
+                stop=True,
+            )
+
+        def half_scores(t, h):
+            score = psum.tile([P, HALF], F32, name="score%d_%d" % (t, h), tag="bank%d" % (t + 4 * h))
+            score_pass(score[:], t, h)
+            start = first[:, t : t + 1] if h else None
+            least = low if h else first
+            nc.vector.tensor_scalar(
+                neg[t][:, HALF * h : HALF * (h + 1)], score[:], -0.03125, start, ALU.mult, ALU.min,
+                accum_out=least[:, t : t + 1],
+            )
+
+        def scores(t):
             score = psum.tile([P, S], F32, name="score%d" % t, tag="bank%d" % t)
             for h in range(2):
-                nc.tensor.matmul_mx(
-                    out=score[:, HALF * h : HALF * (h + 1)],
-                    lhsT=d_key[:, cols].bitcast(FP8X4),
-                    lhsT_scale=planes[:, cols],
-                    rhs=x_g[h][:].bitcast(FP8X4),
-                    rhs_scale=planes[:, S + HALF * h : S + HALF * (h + 1)],
-                    start=True,
-                    stop=True,
-                )
+                score_pass(score[:, HALF * h : HALF * (h + 1)], t, h)
             nc.vector.tensor_scalar(neg[t][:], score[:], -0.03125, None, ALU.mult, ALU.min, accum_out=low[:, t : t + 1])
+
+        def win_exp(t):
             nc.scalar.activation(
                 win[t][:], neg[t][:], ACT.Exp, bias=low[:, t : t + 1], scale=-1.0, accum_out=total[:, t : t + 1]
             )
+
+        def own_dma(t, c, n):
+            tile = sb("own%d_%d" % (t, c), [P, CHUNK * n], F32)
+            nc.sync.dma_start(tile[:], win[t][:, CHUNK * c : CHUNK * (c + n)])
+            for e in range(n):
+                plain[t, c + e] = (tile, e)
 
         def join(t, c, n):
             tile = sb("both%d_%d" % (t, c), [P, CHUNK * n], F32)
@@ -156,9 +184,9 @@ def tile_picked_softkeys_none_po_kernel(
                 both[t, c + e] = (tile, e)
 
         def weigh(t, c, n):
-            if t == 0:
-                rows = sb("z_rows%d" % c, [P, PACK, CHUNK * n], BF16)
-                for e in range(n):
+            if c not in z_rows:
+                rows = sb("z_rows%d" % c, [P, PACK, HALF], BF16)
+                for e in range(2):
                     z_rows[c + e] = (rows, e)
             rows, r = z_rows[c]
             tile, o = both[t, c]
@@ -169,110 +197,130 @@ def tile_picked_softkeys_none_po_kernel(
                 scale=factor[:, t : t + 1],
             )
 
-        def weave_z(c):
+        def weave_z(c, n):
             rows, r = z_rows[c]
+            z_words[c] = sb("z_words%d" % c, [P, CHUNK * n * PACK], BF16)
             nc.vector.tensor_copy(
                 z_words[c][:].rearrange("p (c i t) -> p c t i", t=PACK, i=4),
-                rows[:, :, CHUNK * r : CHUNK * (r + 1)].rearrange("p t (c i) -> p c t i", i=4),
+                rows[:, :, CHUNK * r : CHUNK * (r + n)].rearrange("p t (c i) -> p c t i", i=4),
             )
 
-        def quant_z(c):
-            nc.vector.quantize_mx(out=z_codes[c][:].bitcast(FP8X4), scales=z_scales[c][:], in_=z_words[c][:])
+        def quant_z(c, n):
+            codes = sb("z_codes%d" % c, [P, CHUNK * n], U32)
+            scales = sb("z_scales%d" % c, [P, CHUNK * n], U8)
+            nc.vector.quantize_mx(out=codes[:].bitcast(FP8X4), scales=scales[:], in_=z_words[c][:])
+            z_quant[c] = (codes, scales)
 
-        def product(c, bank):
-            acc = psum.tile([P, PACK, CHUNK], F32, name="acc%d" % bank, tag="bank%d" % bank)
-            for t in range(PACK):
-                nc.tensor.matmul_mx(
-                    out=acc[:, t, :],
-                    lhsT=w_key[:, 2 * P * t : 2 * P * (t + 1)].bitcast(FP4X4),
-                    lhsT_scale=ws_key[:, P * t : P * (t + 1)],
-                    rhs=z_codes[c][:].bitcast(FP8X4),
-                    rhs_scale=z_scales[c][:],
-                    start=True,
-                    stop=True,
-                )
-            return acc
+        def product(c, n, banks):
+            codes, scales = z_quant[c]
+            per = PACK // len(banks)
+            tiles = []
+            for u, bank in enumerate(banks):
+                acc = psum.tile([P, per, CHUNK * n], F32, name="acc%d_%d" % (c, bank), tag="bank%d" % bank)
+                for e in range(per):
+                    t = per * u + e
+                    nc.tensor.matmul_mx(
+                        out=acc[:, e, :],
+                        lhsT=keys["w"][:, 2 * P * t : 2 * P * (t + 1)].bitcast(FP4X4),
+                        lhsT_scale=keys["ws"][:, P * t : P * (t + 1)],
+                        rhs=codes[:].bitcast(FP8X4),
+                        rhs_scale=scales[:],
+                        start=True,
+                        stop=True,
+                    )
+                tiles.append(acc)
+            return tiles
 
-        def empty(c, acc):
-            nc.scalar.copy(y[c][:], acc[:])
-            nc.sync.dma_start(out_rows[:, :, CHUNK * c : CHUNK * (c + 1)], y[c][:])
+        def empty(c, n, tiles):
+            y[c] = sb("y%d" % c, [P, PACK, CHUNK * n], F32)
+            per = PACK // len(tiles)
+            for u, acc in enumerate(tiles):
+                nc.scalar.copy(y[c][:, per * u : per * (u + 1), :], acc[:])
+            nc.sync.dma_start(out_rows[:, :, CHUNK * c : CHUNK * (c + n)], y[c][:])
 
-        def weave_y(c, copy, source):
+        def weave_y(c, n, copy, source):
+            if c < 2:
+                y_words[c] = y_pair[:, CHUNK * PACK * c : CHUNK * PACK * (c + 1)]
+            else:
+                y_words[c] = sb("y_words%d" % c, [P, CHUNK * n * PACK], BF16)[:]
             copy(
-                y_words[c][:].rearrange("p (c i t) -> p c t i", t=PACK, i=4),
+                y_words[c].rearrange("p (c i t) -> p c t i", t=PACK, i=4),
                 source[:].rearrange("p t (c i) -> p c t i", i=4),
             )
 
-        def quant_y(c):
-            cols = slice(CHUNK * c, CHUNK * (c + 1))
-            nc.vector.quantize_mx(out=y_codes[:, cols].bitcast(FP8X4), scales=y_scales[:, cols], in_=y_words[c][:])
-            if c >= 2:
-                pair = slice(0 if c == 2 else CHUNK * c, CHUNK * (c + 1))
-                nc.sync.dma_start(out_codes[:, pair], y_codes[:, pair].bitcast(I32))
+        def quant_y(c, n):
+            cols = slice(CHUNK * c, CHUNK * (c + n))
+            nc.vector.quantize_mx(out=y_codes[:, cols].bitcast(FP8X4), scales=y_scales[:, cols], in_=y_pair[:] if n == 2 else y_words[c])
 
-        scores(0)
-        own_exp(0, 0, 2)
-        scores(1)
-        own_exp(1, 0, 2)
+        def store_codes(c, n):
+            cols = slice(CHUNK * c, CHUNK * (c + n))
+            nc.sync.dma_start(out_codes[:, cols], y_codes[:, cols].bitcast(I32))
+
+        half_scores(0, 0)
+        half_scores(1, 0)
+        half_scores(0, 1)
+        half_scores(1, 1)
         scores(2)
-        own_exp(2, 0, 2)
         scores(3)
+        deal_w()
+        deal_ws()
+        win_exp(0)
+        own_exp(0, 0, 4)
+        win_exp(1)
+        own_exp(1, 0, 4)
+        own_exp(2, 0, 2)
+        win_exp(2)
         own_exp(3, 0, 2)
+        win_exp(3)
+        own_exp(3, 2, 2)
+        own_exp(2, 2, 2)
         join(0, 0, 2)
+        join(0, 2, 2)
         join(1, 0, 2)
+        join(1, 2, 2)
+        nc.vector.reciprocal(inv[:, 0:3], total[:, 0:3])
         join(2, 0, 2)
-        nc.vector.reciprocal(inv[:], total[:])
+        nc.vector.tensor_tensor(factor[:, 0:3], inv[:, 0:3], gn32[:, 0:3], ALU.mult)
+        nc.vector.reciprocal(inv[:, 3:4], total[:, 3:4])
         join(3, 0, 2)
-        nc.vector.tensor_tensor(factor[:], inv[:], gn32[:], ALU.mult)
-        own_exp(0, 2, 2)
-        own_exp(1, 2, 2)
+        nc.vector.tensor_tensor(factor[:, 3:4], inv[:, 3:4], gn32[:, 3:4], ALU.mult)
+        join(3, 2, 2)
         weigh(0, 0, 2)
         weigh(1, 0, 2)
         weigh(2, 0, 2)
         weigh(3, 0, 2)
-        own_exp(2, 2, 2)
-        own_exp(3, 2, 2)
-        join(0, 2, 1)
-        join(1, 2, 1)
-        join(0, 3, 1)
-        weave_z(0)
+        weigh(0, 2, 2)
+        weigh(1, 2, 2)
+        weigh(3, 2, 2)
         join(2, 2, 1)
-        weave_z(1)
-        quant_z(0)
-        acc0 = product(0, 4)
-        join(3, 2, 1)
-        quant_z(1)
-        acc1 = product(1, 5)
-        weigh(0, 2, 1)
-        weigh(1, 2, 1)
-        weigh(2, 2, 1)
-        weigh(3, 2, 1)
-        join(1, 3, 1)
+        weave_z(0, 1)
         join(2, 3, 1)
-        weave_z(2)
-        join(3, 3, 1)
-        quant_z(2)
-        acc2 = product(2, 6)
-        weigh(0, 3, 1)
-        weigh(1, 3, 1)
+        weave_z(1, 1)
+        weigh(2, 2, 1)
         weigh(2, 3, 1)
-        weigh(3, 3, 1)
-        empty(0, acc0)
-        empty(1, acc1)
-        weave_y(0, nc.vector.tensor_copy, y[0])
-        weave_z(3)
-        quant_y(0)
-        quant_z(3)
-        twin3 = product(3, 0)
-        acc3 = product(3, 7)
-        empty(2, acc2)
-        weave_y(1, nc.vector.tensor_copy, y[1])
-        weave_y(2, nc.vector.tensor_copy, y[2])
-        quant_y(1)
-        quant_y(2)
-        weave_y(3, nc.vector.tensor_copy, twin3)
-        empty(3, acc3)
-        quant_y(3)
+        quant_z(0, 1)
+        acc0 = product(0, 1, [4, 5])
+        weave_z(2, 1)
+        quant_z(1, 1)
+        acc1 = product(1, 1, [6, 7])
+        weave_z(3, 1)
+        quant_z(2, 1)
+        acc2 = product(2, 1, [0, 1])
+        quant_z(3, 1)
+        acc3 = product(3, 1, [2, 3])
+        empty(0, 1, acc0)
+        empty(1, 1, acc1)
+        empty(2, 1, acc2)
+        empty(3, 1, acc3)
+        weave_y(0, 1, nc.vector.tensor_copy, y[0])
+        weave_y(1, 1, nc.vector.tensor_copy, y[1])
+        weave_y(2, 1, nc.vector.tensor_copy, y[2])
+        quant_y(0, 2)
+        store_codes(0, 2)
+        weave_y(3, 1, nc.vector.tensor_copy, y[3])
+        quant_y(2, 1)
+        quant_y(3, 1)
+        store_codes(2, 2)
         for q in range(4):
             queue = nc.scalar if q % 2 == 0 else nc.sync
             queue.dma_start(out_2[0][4 * q : 4 * q + 4, :].bitcast(I32), y_scales[32 * q : 32 * q + 4, :].bitcast(I32))

@@ -211,32 +211,39 @@ def tile_picked_softkeys_none_po_kernel(
             nc.vector.quantize_mx(out=codes[:].bitcast(FP8X4), scales=scales[:], in_=z_words[c][:])
             z_quant[c] = (codes, scales)
 
-        def product(c, n, banks):
-            codes, scales = z_quant[c]
-            per = PACK // len(banks)
-            tiles = []
-            for u, bank in enumerate(banks):
-                acc = psum.tile([P, per, CHUNK * n], F32, name="acc%d_%d" % (c, bank), tag="bank%d" % bank)
-                for e in range(per):
-                    t = per * u + e
-                    nc.tensor.matmul_mx(
-                        out=acc[:, e, :],
-                        lhsT=keys["w"][:, 2 * P * t : 2 * P * (t + 1)].bitcast(FP4X4),
-                        lhsT_scale=keys["ws"][:, P * t : P * (t + 1)],
-                        rhs=codes[:].bitcast(FP8X4),
-                        rhs_scale=scales[:],
-                        start=True,
-                        stop=True,
-                    )
-                tiles.append(acc)
-            return tiles
+        y_half = [sb("y_half%d" % h, [P, PACK, HALF], F32) for h in range(2)]
 
-        def empty(c, n, tiles):
-            y[c] = sb("y%d" % c, [P, PACK, CHUNK * n], F32)
-            per = PACK // len(tiles)
-            for u, acc in enumerate(tiles):
-                nc.scalar.copy(y[c][:, per * u : per * (u + 1), :], acc[:])
-            nc.sync.dma_start(out_rows[:, :, CHUNK * c : CHUNK * (c + n)], y[c][:])
+        def product(c, u, acc):
+            codes, scales = z_quant[c]
+            for e in range(2):
+                t = 2 * u + e
+                nc.tensor.matmul_mx(
+                    out=acc[:, e, :],
+                    lhsT=keys["w"][:, 2 * P * t : 2 * P * (t + 1)].bitcast(FP4X4),
+                    lhsT_scale=keys["ws"][:, P * t : P * (t + 1)],
+                    rhs=codes[:].bitcast(FP8X4),
+                    rhs_scale=scales[:],
+                    start=True,
+                    stop=True,
+                )
+
+        def store_y(h, u):
+            nc.sync.dma_start(
+                out_rows[:, 2 * u : 2 * u + 2, HALF * h : HALF * (h + 1)], y_half[h][:, 2 * u : 2 * u + 2, :]
+            )
+
+        def piece(c, u):
+            h, o = divmod(c, 2)
+            acc = psum.tile([P, 2, CHUNK], F32, name="acc%d_%d" % (c, u), tag="bank%d" % ((2 * c + u + 4) % 8))
+            product(c, u, acc)
+            nc.scalar.copy(y_half[h][:, 2 * u : 2 * u + 2, CHUNK * o : CHUNK * (o + 1)], acc[:])
+            if h == 0:
+                nc.sync.dma_start(
+                    out_rows[:, 2 * u : 2 * u + 2, CHUNK * c : CHUNK * (c + 1)],
+                    y_half[0][:, 2 * u : 2 * u + 2, CHUNK * c : CHUNK * (c + 1)],
+                )
+            elif o == 1:
+                store_y(h, u)
 
         def weave_y(c, n, copy, source):
             if c < 2:
@@ -245,7 +252,7 @@ def tile_picked_softkeys_none_po_kernel(
                 y_words[c] = sb("y_words%d" % c, [P, CHUNK * n * PACK], BF16)[:]
             copy(
                 y_words[c].rearrange("p (c i t) -> p c t i", t=PACK, i=4),
-                source[:].rearrange("p t (c i) -> p c t i", i=4),
+                source.rearrange("p t (c i) -> p c t i", i=4),
             )
 
         def quant_y(c, n):
@@ -299,25 +306,20 @@ def tile_picked_softkeys_none_po_kernel(
         weigh(2, 2, 1)
         weigh(2, 3, 1)
         quant_z(0, 1)
-        acc0 = product(0, 1, [4, 5])
         weave_z(2, 1)
         quant_z(1, 1)
-        acc1 = product(1, 1, [6, 7])
         weave_z(3, 1)
         quant_z(2, 1)
-        acc2 = product(2, 1, [0, 1])
         quant_z(3, 1)
-        acc3 = product(3, 1, [2, 3])
-        empty(0, 1, acc0)
-        empty(1, 1, acc1)
-        empty(2, 1, acc2)
-        empty(3, 1, acc3)
-        weave_y(0, 1, nc.vector.tensor_copy, y[0])
-        weave_y(1, 1, nc.vector.tensor_copy, y[1])
-        weave_y(2, 1, nc.vector.tensor_copy, y[2])
+        for c in range(4):
+            for u in range(2):
+                piece(c, u)
+        weave_y(0, 1, nc.vector.tensor_copy, y_half[0][:, :, 0:128])
+        weave_y(1, 1, nc.vector.tensor_copy, y_half[0][:, :, 128:256])
+        weave_y(2, 1, nc.vector.tensor_copy, y_half[1][:, :, 0:128])
         quant_y(0, 2)
         store_codes(0, 2)
-        weave_y(3, 1, nc.vector.tensor_copy, y[3])
+        weave_y(3, 1, nc.vector.tensor_copy, y_half[1][:, :, 128:256])
         quant_y(2, 1)
         quant_y(3, 1)
         store_codes(2, 2)

@@ -110,8 +110,9 @@ def tile_picked_softkeys_none_po_kernel(
         total = sb("total", [P, PACK], F32)
         inv = sb("inv", [P, PACK], F32)
         factor = sb("factor", [P, PACK], F32)
-        neg = [sb("neg%d" % t, [P, S], F32) for t in range(PACK)]
-        win = [sb("win%d" % t, [P, S], F32) for t in range(PACK)]
+        rows = [sb("rows%d" % t, [P, 2 * S if t < 2 else S], F32) for t in range(PACK)]
+        win = [rows[t][:, 0:S] for t in range(PACK)]
+        neg = [rows[t][:, S : 2 * S] if t < 2 else sb("neg%d" % t, [P, S], F32)[:] for t in range(PACK)]
         plain = {}
         both = {}
         z_rows = {}
@@ -161,48 +162,42 @@ def tile_picked_softkeys_none_po_kernel(
             score = psum.tile([P, S], F32, name="score%d" % t, tag="bank%d" % t)
             for h in range(2):
                 score_pass(score[:, HALF * h : HALF * (h + 1)], t, h)
-            nc.vector.tensor_scalar(neg[t][:], score[:], -0.03125, None, ALU.mult, ALU.min, accum_out=low[:, t : t + 1])
+            nc.vector.tensor_scalar(neg[t], score[:], -0.03125, None, ALU.mult, ALU.min, accum_out=low[:, t : t + 1])
 
         def win_exp(t):
             nc.scalar.activation(
-                win[t][:], neg[t][:], ACT.Exp, bias=low[:, t : t + 1], scale=-1.0, accum_out=total[:, t : t + 1]
+                win[t], neg[t], ACT.Exp, bias=low[:, t : t + 1], scale=-1.0, accum_out=total[:, t : t + 1]
             )
-
-        def own_dma(t, c, n):
-            tile = sb("own%d_%d" % (t, c), [P, CHUNK * n], F32)
-            nc.sync.dma_start(tile[:], win[t][:, CHUNK * c : CHUNK * (c + n)])
-            for e in range(n):
-                plain[t, c + e] = (tile, e)
 
         def join(t, c, n):
             tile = sb("both%d_%d" % (t, c), [P, CHUNK * n], F32)
             own, o = plain[t, c]
             nc.vector.tensor_tensor(
-                tile[:], win[t][:].indirect(nb_sb[:, 8 * c : 8 * (c + n)]), own[:, CHUNK * o : CHUNK * (o + n)], ALU.add
+                tile[:], rows[t][:].indirect(nb_sb[:, 8 * c : 8 * (c + n)]), own[:, CHUNK * o : CHUNK * (o + n)], ALU.add
             )
             for e in range(n):
                 both[t, c + e] = (tile, e)
 
         def weigh(t, c, n):
             if c not in z_rows:
-                rows = sb("z_rows%d" % c, [P, PACK, HALF], BF16)
+                zr = sb("z_rows%d" % c, [P, PACK, HALF], BF16)
                 for e in range(2):
-                    z_rows[c + e] = (rows, e)
-            rows, r = z_rows[c]
+                    z_rows[c + e] = (zr, e)
+            zr, r = z_rows[c]
             tile, o = both[t, c]
             nc.scalar.activation(
-                rows[:, t, CHUNK * r : CHUNK * (r + n)],
+                zr[:, t, CHUNK * r : CHUNK * (r + n)],
                 tile[:, CHUNK * o : CHUNK * (o + n)],
                 ACT.Copy,
                 scale=factor[:, t : t + 1],
             )
 
         def weave_z(c, n):
-            rows, r = z_rows[c]
+            zr, r = z_rows[c]
             z_words[c] = sb("z_words%d" % c, [P, CHUNK * n * PACK], BF16)
             nc.vector.tensor_copy(
                 z_words[c][:].rearrange("p (c i t) -> p c t i", t=PACK, i=4),
-                rows[:, :, CHUNK * r : CHUNK * (r + n)].rearrange("p t (c i) -> p c t i", i=4),
+                zr[:, :, CHUNK * r : CHUNK * (r + n)].rearrange("p t (c i) -> p c t i", i=4),
             )
 
         def quant_z(c, n):
@@ -227,9 +222,10 @@ def tile_picked_softkeys_none_po_kernel(
                     stop=True,
                 )
 
-        def store_y(h, u):
+        def store_y(c, a, b):
+            h, o = divmod(c, 2)
             nc.sync.dma_start(
-                out_rows[:, 2 * u : 2 * u + 2, HALF * h : HALF * (h + 1)], y_half[h][:, 2 * u : 2 * u + 2, :]
+                out_rows[:, a:b, CHUNK * c : CHUNK * (c + 1)], y_half[h][:, a:b, CHUNK * o : CHUNK * (o + 1)]
             )
 
         def piece(c, u):
@@ -237,13 +233,10 @@ def tile_picked_softkeys_none_po_kernel(
             acc = psum.tile([P, 2, CHUNK], F32, name="acc%d_%d" % (c, u), tag="bank%d" % ((2 * c + u + 4) % 8))
             product(c, u, acc)
             nc.scalar.copy(y_half[h][:, 2 * u : 2 * u + 2, CHUNK * o : CHUNK * (o + 1)], acc[:])
-            if h == 0:
-                nc.sync.dma_start(
-                    out_rows[:, 2 * u : 2 * u + 2, CHUNK * c : CHUNK * (c + 1)],
-                    y_half[0][:, 2 * u : 2 * u + 2, CHUNK * c : CHUNK * (c + 1)],
-                )
-            elif o == 1:
-                store_y(h, u)
+            if c == 0:
+                store_y(c, 2 * u, 2 * u + 2)
+            elif u == 1:
+                store_y(c, 0, PACK)
 
         def weave_y(c, n, copy, source):
             if c < 2:
@@ -281,10 +274,8 @@ def tile_picked_softkeys_none_po_kernel(
         win_exp(3)
         own_exp(3, 2, 2)
         own_exp(2, 2, 2)
-        join(0, 0, 2)
-        join(0, 2, 2)
-        join(1, 0, 2)
-        join(1, 2, 2)
+        join(0, 0, 4)
+        join(1, 0, 4)
         nc.vector.reciprocal(inv[:, 0:3], total[:, 0:3])
         join(2, 0, 2)
         nc.vector.tensor_tensor(factor[:, 0:3], inv[:, 0:3], gn32[:, 0:3], ALU.mult)

@@ -222,10 +222,9 @@ def tile_picked_softkeys_none_po_kernel(
                     stop=True,
                 )
 
-        def store_y(c, a, b):
-            h, o = divmod(c, 2)
+        def store_y(h, u):
             nc.sync.dma_start(
-                out_rows[:, a:b, CHUNK * c : CHUNK * (c + 1)], y_half[h][:, a:b, CHUNK * o : CHUNK * (o + 1)]
+                out_rows[:, 2 * u : 2 * u + 2, HALF * h : HALF * (h + 1)], y_half[h][:, 2 * u : 2 * u + 2, :]
             )
 
         def piece(c, u):
@@ -233,10 +232,13 @@ def tile_picked_softkeys_none_po_kernel(
             acc = psum.tile([P, 2, CHUNK], F32, name="acc%d_%d" % (c, u), tag="bank%d" % ((2 * c + u + 4) % 8))
             product(c, u, acc)
             nc.scalar.copy(y_half[h][:, 2 * u : 2 * u + 2, CHUNK * o : CHUNK * (o + 1)], acc[:])
-            if c == 0:
-                store_y(c, 2 * u, 2 * u + 2)
-            elif u == 1:
-                store_y(c, 0, PACK)
+            if h == 0:
+                nc.sync.dma_start(
+                    out_rows[:, 2 * u : 2 * u + 2, CHUNK * c : CHUNK * (c + 1)],
+                    y_half[0][:, 2 * u : 2 * u + 2, CHUNK * c : CHUNK * (c + 1)],
+                )
+            elif o == 1:
+                store_y(h, u)
 
         def weave_y(c, n, copy, source):
             if c < 2:

@@ -192,10 +192,10 @@ def tile_picked_softkeys_none_po_kernel(
                 scale=factor[:, t : t + 1],
             )
 
-        def weave_z(c, n):
+        def weave_z(c, n, copy=nc.vector.tensor_copy):
             zr, r = z_rows[c]
             z_words[c] = sb("z_words%d" % c, [P, CHUNK * n * PACK], BF16)
-            nc.vector.tensor_copy(
+            copy(
                 z_words[c][:].rearrange("p (c i t) -> p c t i", t=PACK, i=4),
                 zr[:, :, CHUNK * r : CHUNK * (r + n)].rearrange("p t (c i) -> p c t i", i=4),
             )
@@ -274,8 +274,8 @@ def tile_picked_softkeys_none_po_kernel(
         win_exp(2)
         own_exp(3, 0, 2)
         win_exp(3)
-        own_exp(3, 2, 2)
         own_exp(2, 2, 2)
+        own_exp(3, 2, 2)
         join(0, 0, 4)
         join(1, 0, 4)
         nc.vector.reciprocal(inv[:, 0:3], total[:, 0:3])
@@ -284,34 +284,35 @@ def tile_picked_softkeys_none_po_kernel(
         nc.vector.reciprocal(inv[:, 3:4], total[:, 3:4])
         join(3, 0, 2)
         nc.vector.tensor_tensor(factor[:, 3:4], inv[:, 3:4], gn32[:, 3:4], ALU.mult)
-        join(3, 2, 2)
+        join(2, 2, 2)
         weigh(0, 0, 2)
         weigh(1, 0, 2)
         weigh(2, 0, 2)
         weigh(3, 0, 2)
         weigh(0, 2, 2)
         weigh(1, 2, 2)
-        weigh(3, 2, 2)
-        join(2, 2, 1)
+        weigh(2, 2, 2)
+        join(3, 2, 2)
         weave_z(0, 1)
-        join(2, 3, 1)
         weave_z(1, 1)
-        weigh(2, 2, 1)
-        weigh(2, 3, 1)
+        weigh(3, 2, 2)
         quant_z(0, 1)
         weave_z(2, 1)
         quant_z(1, 1)
-        weave_z(3, 1)
+        weave_z(3, 1, nc.scalar.copy)
         quant_z(2, 1)
         quant_z(3, 1)
-        for c in range(4):
+        for c in range(2):
             for u in range(2):
+                piece(c, u)
+        for u in range(2):
+            for c in range(2, 4):
                 piece(c, u)
         weave_y(0, 1, nc.vector.tensor_copy, y_half[0][:, :, 0:128])
         weave_y(1, 1, nc.vector.tensor_copy, y_half[0][:, :, 128:256])
-        weave_y(2, 1, nc.vector.tensor_copy, y_half[1][:, :, 0:128])
         quant_y(0, 2)
         store_codes(0, 2)
+        weave_y(2, 1, nc.vector.tensor_copy, y_half[1][:, :, 0:128])
         weave_y(3, 1, nc.vector.tensor_copy, y_half[1][:, :, 128:256])
         quant_y(2, 1)
         quant_y(3, 1)

@@ -40,7 +40,7 @@ def tile_picked_softkeys_none_po_kernel(
         kidx_sb = sb("kidx_sb", [P, S // 16], U16)
         offs_sb = sb("offs_sb", [P, S // 16], U16)
         nb_sb = sb("nb_sb", [P, S // 16], U16)
-        d_tab = sb("d_tab", [P, TABLE], U32)
+        d_tab = sb_at("d_tab", [P, TABLE], U32, 20480)
         x_tab = sb_at("x_tab", [P, TABLE], U32, 4096)
         ds_tab = sb_at("ds_tab", [P, TABLE], U8, 16384)
         xs_tab = sb("xs_tab", [P, TABLE], U8)
@@ -75,17 +75,23 @@ def tile_picked_softkeys_none_po_kernel(
             nc.scalar.dma_start(planes[j:P:32, :].bitcast(I32), planes[8 * j : P : 32, :].bitcast(I32))
         w_raw = sb_at("w_raw", [P, 2 * S], U8, 0)
         nc.sync.dma_start(w_raw[:].bitcast(I32), w1_words[0].bitcast(I32))
-        ws_raw = sb_at("ws_raw", [P, S], U8, 1024)
+        d_g = [sb("d_g%d" % h, [P, HALF], U32) for h in range(2)]
+        d_key = sb_at("d_key", [P, S], U32, 2048)
+        for h in range(2):
+            nc.vector.tensor_copy(d_g[h][:], d_tab[:].indirect(kidx_sb[:, 16 * h : 16 * (h + 1)]))
+
+        def deal_keys(h):
+            nc.vector.tensor_copy(
+                d_key[:].bitcast(I32).rearrange("p (t c i) -> p c t i", t=PACK, i=4)[:, 16 * h : 16 * (h + 1)],
+                d_g[h][:].bitcast(I32).rearrange("p (c i t) -> p c t i", t=PACK, i=4),
+            )
+
+        deal_keys(0)
+        ws_raw = sb_at("ws_raw", [P, S], U8, 20480)
         nc.vector.memset(ws_raw[:].bitcast(I32), 0)
+        deal_keys(1)
         for a in range(4):
             nc.sync.dma_start(ws_raw[a:P:32, :].bitcast(I32), w1_scales[0][a:16:4, :].bitcast(I32))
-        d_g = sb("d_g", [P, S], U32)
-        d_key = sb_at("d_key", [P, S], U32, 2048)
-        nc.vector.tensor_copy(d_g[:], d_tab[:].indirect(kidx_sb[:]))
-        nc.vector.tensor_copy(
-            d_key[:].bitcast(I32).rearrange("p (t c i) -> p c t i", t=PACK, i=4),
-            d_g[:].bitcast(I32).rearrange("p (c i t) -> p c t i", t=PACK, i=4),
-        )
         x_g = [sb("x_g%d" % h, [P, HALF], U32) for h in range(2)]
         for h in range(2):
             nc.vector.tensor_copy(x_g[h][:], x_tab[:].indirect(offs_sb[:, 16 * h : 16 * (h + 1)]))
@@ -192,10 +198,10 @@ def tile_picked_softkeys_none_po_kernel(
                 scale=factor[:, t : t + 1],
             )
 
-        def weave_z(c, n, copy=nc.vector.tensor_copy):
+        def weave_z(c, n):
             zr, r = z_rows[c]
             z_words[c] = sb("z_words%d" % c, [P, CHUNK * n * PACK], BF16)
-            copy(
+            nc.vector.tensor_copy(
                 z_words[c][:].rearrange("p (c i t) -> p c t i", t=PACK, i=4),
                 zr[:, :, CHUNK * r : CHUNK * (r + n)].rearrange("p t (c i) -> p c t i", i=4),
             )
@@ -208,12 +214,13 @@ def tile_picked_softkeys_none_po_kernel(
 
         y_half = [sb("y_half%d" % h, [P, PACK, HALF], F32) for h in range(2)]
 
-        def product(c, u, acc):
+        def piece(n, c, a, b):
+            h, o = divmod(c, 2)
             codes, scales = z_quant[c]
-            for e in range(2):
-                t = 2 * u + e
+            acc = psum.tile([P, b - a, CHUNK], F32, name="acc%d" % n, tag="bank%d" % ((n + 4) % 8))
+            for t in range(a, b):
                 nc.tensor.matmul_mx(
-                    out=acc[:, e, :],
+                    out=acc[:, t - a, :],
                     lhsT=keys["w"][:, 2 * P * t : 2 * P * (t + 1)].bitcast(FP4X4),
                     lhsT_scale=keys["ws"][:, P * t : P * (t + 1)],
                     rhs=codes[:].bitcast(FP8X4),
@@ -221,24 +228,13 @@ def tile_picked_softkeys_none_po_kernel(
                     start=True,
                     stop=True,
                 )
-
-        def store_y(h, u):
-            nc.sync.dma_start(
-                out_rows[:, 2 * u : 2 * u + 2, HALF * h : HALF * (h + 1)], y_half[h][:, 2 * u : 2 * u + 2, :]
-            )
-
-        def piece(c, u):
-            h, o = divmod(c, 2)
-            acc = psum.tile([P, 2, CHUNK], F32, name="acc%d_%d" % (c, u), tag="bank%d" % ((2 * c + u + 4) % 8))
-            product(c, u, acc)
-            nc.scalar.copy(y_half[h][:, 2 * u : 2 * u + 2, CHUNK * o : CHUNK * (o + 1)], acc[:])
+            nc.scalar.copy(y_half[h][:, a:b, CHUNK * o : CHUNK * (o + 1)], acc[:])
             if h == 0:
                 nc.sync.dma_start(
-                    out_rows[:, 2 * u : 2 * u + 2, CHUNK * c : CHUNK * (c + 1)],
-                    y_half[0][:, 2 * u : 2 * u + 2, CHUNK * c : CHUNK * (c + 1)],
+                    out_rows[:, a:b, CHUNK * c : CHUNK * (c + 1)], y_half[0][:, a:b, CHUNK * c : CHUNK * (c + 1)]
                 )
             elif o == 1:
-                store_y(h, u)
+                nc.sync.dma_start(out_rows[:, a:b, HALF:S], y_half[1][:, a:b, :])
 
         def weave_y(c, n, copy, source):
             if c < 2:
@@ -274,8 +270,8 @@ def tile_picked_softkeys_none_po_kernel(
         win_exp(2)
         own_exp(3, 0, 2)
         win_exp(3)
-        own_exp(2, 2, 2)
         own_exp(3, 2, 2)
+        own_exp(2, 2, 2)
         join(0, 0, 4)
         join(1, 0, 4)
         nc.vector.reciprocal(inv[:, 0:3], total[:, 0:3])
@@ -284,35 +280,34 @@ def tile_picked_softkeys_none_po_kernel(
         nc.vector.reciprocal(inv[:, 3:4], total[:, 3:4])
         join(3, 0, 2)
         nc.vector.tensor_tensor(factor[:, 3:4], inv[:, 3:4], gn32[:, 3:4], ALU.mult)
-        join(2, 2, 2)
+        join(3, 2, 2)
         weigh(0, 0, 2)
         weigh(1, 0, 2)
         weigh(2, 0, 2)
         weigh(3, 0, 2)
         weigh(0, 2, 2)
         weigh(1, 2, 2)
-        weigh(2, 2, 2)
-        join(3, 2, 2)
-        weave_z(0, 1)
-        weave_z(1, 1)
         weigh(3, 2, 2)
+        join(2, 2, 1)
+        weave_z(0, 1)
+        join(2, 3, 1)
+        weave_z(1, 1)
+        weigh(2, 2, 1)
+        weigh(2, 3, 1)
         quant_z(0, 1)
         weave_z(2, 1)
         quant_z(1, 1)
-        weave_z(3, 1, nc.scalar.copy)
+        weave_z(3, 1)
         quant_z(2, 1)
         quant_z(3, 1)
-        for c in range(2):
-            for u in range(2):
-                piece(c, u)
-        for u in range(2):
-            for c in range(2, 4):
-                piece(c, u)
+        pieces = [(c, a, a + 2) for c in range(4) for a in (0, 2)]
+        for n, (c, a, b) in enumerate(pieces):
+            piece(n, c, a, b)
         weave_y(0, 1, nc.vector.tensor_copy, y_half[0][:, :, 0:128])
         weave_y(1, 1, nc.vector.tensor_copy, y_half[0][:, :, 128:256])
+        weave_y(2, 1, nc.vector.tensor_copy, y_half[1][:, :, 0:128])
         quant_y(0, 2)
         store_codes(0, 2)
-        weave_y(2, 1, nc.vector.tensor_copy, y_half[1][:, :, 0:128])
         weave_y(3, 1, nc.vector.tensor_copy, y_half[1][:, :, 128:256])
         quant_y(2, 1)
         quant_y(3, 1)

@@ -99,10 +99,10 @@ def tile_picked_softkeys_none_po_kernel(
         keys = {}
 
         def deal_w():
-            keys["w"] = sb_at("w_key", [P, 2 * S], U8, 4096)
-            nc.gpsimd.tensor_copy(
-                keys["w"][:].rearrange("p (t c i b) -> p c t i b", t=PACK, i=8, b=2),
-                w_raw[:].rearrange("p (c i t b) -> p c t i b", t=PACK, i=8, b=2),
+            keys["w"] = sb("w_key", [P, 2 * S], U8)
+            nc.scalar.copy(
+                keys["w"][:].bitcast(U16).rearrange("p (t c i) -> p c t i", t=PACK, i=8),
+                w_raw[:].bitcast(U16).rearrange("p (c i t) -> p c t i", t=PACK, i=8),
             )
 
         def deal_ws():

@@ -98,12 +98,13 @@ def tile_picked_softkeys_none_po_kernel(
 
         keys = {}
 
-        def deal_w():
-            keys["w"] = sb("w_key", [P, 2 * S], U8)
+        def deal_w(tile, a, b):
             nc.scalar.copy(
-                keys["w"][:].bitcast(U16).rearrange("p (t c i) -> p c t i", t=PACK, i=8),
-                w_raw[:].bitcast(U16).rearrange("p (c i t) -> p c t i", t=PACK, i=8),
+                tile[:].bitcast(U16).rearrange("p (t c i) -> p c t i", t=b - a, i=8),
+                w_raw[:].bitcast(U16).rearrange("p (c i t) -> p c t i", t=PACK, i=8)[:, :, a:b, :],
             )
+            for t in range(a, b):
+                keys[t] = tile[:, 2 * P * (t - a) : 2 * P * (t - a + 1)]
 
         def deal_ws():
             keys["ws"] = sb_at("ws_key", [P, S], U8, 4096 + 2 * S)
@@ -133,7 +134,10 @@ def tile_picked_softkeys_none_po_kernel(
         out_codes = out_1[0].rearrange("p n t -> p (n t)").bitcast(I32)
 
         def own_exp(t, c, n):
-            tile = sb("own%d_%d" % (t, c), [P, CHUNK * n], F32)
+            if (t, c) == (3, 2):
+                tile = sb_at("own3_2", [P, CHUNK * n], F32, 32768)
+            else:
+                tile = sb("own%d_%d" % (t, c), [P, CHUNK * n], F32)
             nc.scalar.activation(
                 tile[:], neg[t][:, CHUNK * c : CHUNK * (c + n)], ACT.Exp, bias=low[:, t : t + 1], scale=-1.0
             )
@@ -221,7 +225,7 @@ def tile_picked_softkeys_none_po_kernel(
             for t in range(a, b):
                 nc.tensor.matmul_mx(
                     out=acc[:, t - a, :],
-                    lhsT=keys["w"][:, 2 * P * t : 2 * P * (t + 1)].bitcast(FP4X4),
+                    lhsT=keys[t].bitcast(FP4X4),
                     lhsT_scale=keys["ws"][:, P * t : P * (t + 1)],
                     rhs=codes[:].bitcast(FP8X4),
                     rhs_scale=scales[:],
@@ -260,7 +264,7 @@ def tile_picked_softkeys_none_po_kernel(
         half_scores(1, 1)
         scores(2)
         scores(3)
-        deal_w()
+        deal_w(sb("w_key", [P, 2 * P * 3], U8), 0, 3)
         deal_ws()
         win_exp(0)
         own_exp(0, 0, 4)
@@ -286,6 +290,18 @@ def tile_picked_softkeys_none_po_kernel(
         weigh(2, 0, 2)
         weigh(3, 0, 2)
         weigh(0, 2, 2)
+        deal_w(sb_at("w_last", [P, 2 * P], U8, 32768), 3, 4)
+        idle = psum.tile([P, HALF + CHUNK], F32, name="idle", tag="bank3")
+        for a, b in ((0, HALF), (0, CHUNK)):
+            nc.tensor.matmul_mx(
+                out=idle[:, HALF - b : HALF] if b == HALF else idle[:, HALF : HALF + b],
+                lhsT=keys[3].bitcast(FP4X4),
+                lhsT_scale=keys["ws"][:, 3 * P : 4 * P],
+                rhs=d_key[:, a:b].bitcast(FP8X4),
+                rhs_scale=planes[:, a:b],
+                start=True,
+                stop=True,
+            )
         weigh(1, 2, 2)
         weigh(3, 2, 2)
         join(2, 2, 1)

@@ -96,55 +96,39 @@ def tile_picked_softkeys_none_po_kernel(
         for h in range(2):
             nc.vector.tensor_copy(x_g[h][:], x_tab[:].indirect(offs_sb[:, 16 * h : 16 * (h + 1)]))
 
-        keys = {}
-
-        def deal_w(tile, a, b):
-            nc.scalar.copy(
-                tile[:].bitcast(U16).rearrange("p (t c i) -> p c t i", t=b - a, i=8),
-                w_raw[:].bitcast(U16).rearrange("p (c i t) -> p c t i", t=PACK, i=8)[:, :, a:b, :],
-            )
-            for t in range(a, b):
-                keys[t] = tile[:, 2 * P * (t - a) : 2 * P * (t - a + 1)]
-
-        def deal_ws():
-            keys["ws"] = sb_at("ws_key", [P, S], U8, 4096 + 2 * S)
-            nc.gpsimd.tensor_copy(
-                keys["ws"][:].rearrange("p (t c i) -> p c t i", t=PACK, i=16),
-                ws_raw[:].rearrange("p (c i t) -> p c t i", t=PACK, i=16),
-            )
-
-        low = sb("low", [P, PACK], F32)
-        total = sb("total", [P, PACK], F32)
-        inv = sb("inv", [P, PACK], F32)
-        factor = sb("factor", [P, PACK], F32)
-        rows = [sb("rows%d" % t, [P, 2 * S if t < 2 else S], F32) for t in range(PACK)]
-        win = [rows[t][:, 0:S] for t in range(PACK)]
-        neg = [rows[t][:, S : 2 * S] if t < 2 else sb("neg%d" % t, [P, S], F32)[:] for t in range(PACK)]
-        plain = {}
-        both = {}
-        z_rows = {}
-        z_words = {}
-        z_quant = {}
-        y = {}
-        y_words = {}
-        y_pair = sb("y_pair", [P, HALF * PACK], BF16)
-        y_codes = sb("y_codes", [P, S], U32)
-        y_scales = sb("y_scales", [P, S], U8)
-        out_rows = out_0.rearrange("(p t) n -> p t n", t=PACK)
-        out_codes = out_1[0].rearrange("p n t -> p (n t)").bitcast(I32)
-
-        def own_exp(t, c, n):
-            if (t, c) == (3, 2):
-                tile = sb_at("own3_2", [P, CHUNK * n], F32, 32768)
-            else:
-                tile = sb("own%d_%d" % (t, c), [P, CHUNK * n], F32)
-            nc.scalar.activation(
-                tile[:], neg[t][:, CHUNK * c : CHUNK * (c + n)], ACT.Exp, bias=low[:, t : t + 1], scale=-1.0
-            )
-            for e in range(n):
-                plain[t, c + e] = (tile, e)
+        w_key = sb_at("w_key", [P, 2 * S], U8, 4096)
+        nc.gpsimd.tensor_copy(
+            w_key[:].rearrange("p (t m b) -> p t m b", t=PACK, b=2),
+            w_raw[:].rearrange("p (m t b) -> p t m b", t=PACK, b=2),
+        )
+        ws_key = sb_at("ws_key", [P, S], U8, 4096 + 2 * S)
+        nc.gpsimd.tensor_copy(
+            ws_key[:].rearrange("p (t c i) -> p c t i", t=PACK, i=16),
+            ws_raw[:].rearrange("p (c i t) -> p c t i", t=PACK, i=16),
+        )
 
         first = sb("first", [P, PACK], F32)
+        low = sb("low", [P, PACK], F32)
+        total = sb("total", [P, PACK], F32)
+        inv = sb("inv", [P, 2], F32)
+        factor = sb("factor", [P, PACK], F32)
+        neg = [sb("neg%d" % t, [P, S], F32) for t in range(PACK)]
+        win = [sb("win%d" % t, [P, S], F32) for t in range(PACK)]
+        plain = sb_at("plain", [P, PACK, S], F32, 45056)
+        gain = sb("gain", [P, HALF], F32)
+        nc.scalar.activation(gain[:], gn32[:, 0:1].to_broadcast([P, HALF]), ACT.Copy)
+        spread = sb("spread", [P, HALF], F32)
+        last_inv = sb_at("last_inv", [P, 1], F32, 36864)
+        mid_inv = sb_at("mid_inv", [P, 1], F32, 53248)
+        picked = {}
+        z_words = {}
+        z_quant = {}
+        y_words = {}
+        y_codes = sb("y_codes", [P, S], U32)
+        y_scales = sb("y_scales", [P, S], U8)
+        y_half = [sb("y_half%d" % h, [P, PACK, HALF], F32) for h in range(2)]
+        out_rows = out_0.rearrange("(p t) n -> p t n", t=PACK)
+        out_codes = out_1[0].rearrange("p n t -> p (n t)").bitcast(I32)
 
         def score_pass(out, t, h):
             cols = slice(P * t, P * (t + 1))
@@ -172,51 +156,65 @@ def tile_picked_softkeys_none_po_kernel(
             score = psum.tile([P, S], F32, name="score%d" % t, tag="bank%d" % t)
             for h in range(2):
                 score_pass(score[:, HALF * h : HALF * (h + 1)], t, h)
-            nc.vector.tensor_scalar(neg[t], score[:], -0.03125, None, ALU.mult, ALU.min, accum_out=low[:, t : t + 1])
+            nc.vector.tensor_scalar(neg[t][:], score[:], -0.03125, None, ALU.mult, ALU.min, accum_out=low[:, t : t + 1])
 
-        def win_exp(t):
+        def exp_row(t):
             nc.scalar.activation(
-                win[t], neg[t], ACT.Exp, bias=low[:, t : t + 1], scale=-1.0, accum_out=total[:, t : t + 1]
+                win[t][:], neg[t][:], ACT.Exp, bias=low[:, t : t + 1], scale=-1.0, accum_out=total[:, t : t + 1]
             )
 
-        def join(t, c, n):
-            tile = sb("both%d_%d" % (t, c), [P, CHUNK * n], F32)
-            own, o = plain[t, c]
+        def inverse(a, b):
+            return {0: inv[:, 0:1], 1: mid_inv[:], 2: inv[:, 1:2], 3: last_inv[:]}[a]
+
+        def invert(a, b):
+            nc.vector.reciprocal(inverse(a, b), total[:, a:b])
+
+        def make_factor(a, b):
+            nc.vector.tensor_tensor(factor[:, a:b], inverse(a, b), gn32[:, a:b], ALU.mult)
+
+        def by_row(t):
+            return spread[:, 0:1] if t == 0 else factor[:, t : t + 1]
+
+        def weigh(t):
+            nc.vector.tensor_scalar(plain[:, t, :], win[t][:], by_row(t), None, ALU.mult)
+
+        def slot(t, c, n):
+            if c not in picked:
+                if c == 0:
+                    tile = sb_at("picked0", [P, PACK, HALF], F32, 53248)
+                    picked[0] = tile[:, :, 0:CHUNK]
+                    picked[1] = tile[:, :, CHUNK:HALF]
+                    picked["half"] = tile
+                else:
+                    late = sb_at("picked_late", [P, 2, PACK, CHUNK], F32, 36864)
+                    picked[2] = late[:, 0]
+                    picked[3] = late[:, 1]
+            return picked["half"][:, t, :] if n == 2 else picked[c][:, t, :]
+
+        def pick_scalar(t, c, n):
+            nc.scalar.activation(
+                slot(t, c, n), win[t][:].indirect(nb_sb[:, 8 * c : 8 * (c + n)]), ACT.Copy, scale=by_row(t)
+            )
+
+        def pick_vector(t, c, n):
             nc.vector.tensor_tensor(
-                tile[:], rows[t][:].indirect(nb_sb[:, 8 * c : 8 * (c + n)]), own[:, CHUNK * o : CHUNK * (o + n)], ALU.add
-            )
-            for e in range(n):
-                both[t, c + e] = (tile, e)
-
-        def weigh(t, c, n):
-            if c not in z_rows:
-                zr = sb("z_rows%d" % c, [P, PACK, HALF], BF16)
-                for e in range(2):
-                    z_rows[c + e] = (zr, e)
-            zr, r = z_rows[c]
-            tile, o = both[t, c]
-            nc.scalar.activation(
-                zr[:, t, CHUNK * r : CHUNK * (r + n)],
-                tile[:, CHUNK * o : CHUNK * (o + n)],
-                ACT.Copy,
-                scale=factor[:, t : t + 1],
+                slot(t, c, n), win[t][:].indirect(nb_sb[:, 8 * c : 8 * (c + n)]), spread[:, 0 : CHUNK * n], ALU.mult
             )
 
-        def weave_z(c, n):
-            zr, r = z_rows[c]
-            z_words[c] = sb("z_words%d" % c, [P, CHUNK * n * PACK], BF16)
-            nc.vector.tensor_copy(
-                z_words[c][:].rearrange("p (c i t) -> p c t i", t=PACK, i=4),
-                zr[:, :, CHUNK * r : CHUNK * (r + n)].rearrange("p t (c i) -> p c t i", i=4),
+        def weave_z(c):
+            z_words[c] = sb_at("z_words%d" % c, [P, CHUNK * PACK], BF16, 40960 + 1024 * (c % 2))
+            nc.vector.tensor_tensor(
+                z_words[c][:].rearrange("p (c t) -> p c t", t=PACK),
+                plain[:, :, CHUNK * c : CHUNK * (c + 1)].rearrange("p t c -> p c t"),
+                picked[c].rearrange("p t c -> p c t"),
+                ALU.add,
             )
 
-        def quant_z(c, n):
-            codes = sb("z_codes%d" % c, [P, CHUNK * n], U32)
-            scales = sb("z_scales%d" % c, [P, CHUNK * n], U8)
+        def quant_z(c):
+            codes = sb("z_codes%d" % c, [P, CHUNK], U32)
+            scales = sb("z_scales%d" % c, [P, CHUNK], U8)
             nc.vector.quantize_mx(out=codes[:].bitcast(FP8X4), scales=scales[:], in_=z_words[c][:])
             z_quant[c] = (codes, scales)
-
-        y_half = [sb("y_half%d" % h, [P, PACK, HALF], F32) for h in range(2)]
 
         def piece(n, c, a, b):
             h, o = divmod(c, 2)
@@ -225,8 +223,8 @@ def tile_picked_softkeys_none_po_kernel(
             for t in range(a, b):
                 nc.tensor.matmul_mx(
                     out=acc[:, t - a, :],
-                    lhsT=keys[t].bitcast(FP4X4),
-                    lhsT_scale=keys["ws"][:, P * t : P * (t + 1)],
+                    lhsT=w_key[:, 2 * P * t : 2 * P * (t + 1)].bitcast(FP4X4),
+                    lhsT_scale=ws_key[:, P * t : P * (t + 1)],
                     rhs=codes[:].bitcast(FP8X4),
                     rhs_scale=scales[:],
                     start=True,
@@ -240,19 +238,28 @@ def tile_picked_softkeys_none_po_kernel(
             elif o == 1:
                 nc.sync.dma_start(out_rows[:, a:b, HALF:S], y_half[1][:, a:b, :])
 
-        def weave_y(c, n, copy, source):
+        def product(c):
+            piece(2 * c, c, 0, 2)
+            piece(2 * c + 1, c, 2, 4)
+
+        def weave_y(c):
+            h, o = divmod(c, 2)
+            if c == 0:
+                y_words["pair"] = sb_at("y_pair", [P, HALF * PACK], BF16, 45056)
             if c < 2:
-                y_words[c] = y_pair[:, CHUNK * PACK * c : CHUNK * PACK * (c + 1)]
+                y_words[c] = y_words["pair"][:, CHUNK * PACK * c : CHUNK * PACK * (c + 1)]
             else:
-                y_words[c] = sb("y_words%d" % c, [P, CHUNK * n * PACK], BF16)[:]
-            copy(
+                y_words[c] = sb("y_words%d" % c, [P, CHUNK * PACK], BF16)[:]
+            nc.vector.tensor_copy(
                 y_words[c].rearrange("p (c i t) -> p c t i", t=PACK, i=4),
-                source.rearrange("p t (c i) -> p c t i", i=4),
+                y_half[h][:, :, CHUNK * o : CHUNK * (o + 1)].rearrange("p t (c i) -> p c t i", i=4),
             )
 
         def quant_y(c, n):
             cols = slice(CHUNK * c, CHUNK * (c + n))
-            nc.vector.quantize_mx(out=y_codes[:, cols].bitcast(FP8X4), scales=y_scales[:, cols], in_=y_pair[:] if n == 2 else y_words[c])
+            nc.vector.quantize_mx(
+                out=y_codes[:, cols].bitcast(FP8X4), scales=y_scales[:, cols], in_=y_words["pair"][:] if n == 2 else y_words[c]
+            )
 
         def store_codes(c, n):
             cols = slice(CHUNK * c, CHUNK * (c + n))
@@ -261,70 +268,50 @@ def tile_picked_softkeys_none_po_kernel(
         half_scores(0, 0)
         half_scores(1, 0)
         half_scores(0, 1)
+        exp_row(0)
         half_scores(1, 1)
+        exp_row(1)
         scores(2)
+        exp_row(2)
+        invert(0, 1)
         scores(3)
-        deal_w(sb("w_key", [P, 2 * P * 3], U8), 0, 3)
-        deal_ws()
-        win_exp(0)
-        own_exp(0, 0, 4)
-        win_exp(1)
-        own_exp(1, 0, 4)
-        own_exp(2, 0, 2)
-        win_exp(2)
-        own_exp(3, 0, 2)
-        win_exp(3)
-        own_exp(3, 2, 2)
-        own_exp(2, 2, 2)
-        join(0, 0, 4)
-        join(1, 0, 4)
-        nc.vector.reciprocal(inv[:, 0:3], total[:, 0:3])
-        join(2, 0, 2)
-        nc.vector.tensor_tensor(factor[:, 0:3], inv[:, 0:3], gn32[:, 0:3], ALU.mult)
-        nc.vector.reciprocal(inv[:, 3:4], total[:, 3:4])
-        join(3, 0, 2)
-        nc.vector.tensor_tensor(factor[:, 3:4], inv[:, 3:4], gn32[:, 3:4], ALU.mult)
-        join(3, 2, 2)
-        weigh(0, 0, 2)
-        weigh(1, 0, 2)
-        weigh(2, 0, 2)
-        weigh(3, 0, 2)
-        weigh(0, 2, 2)
-        deal_w(sb_at("w_last", [P, 2 * P], U8, 32768), 3, 4)
-        idle = psum.tile([P, HALF + CHUNK], F32, name="idle", tag="bank3")
-        for a, b in ((0, HALF), (0, CHUNK)):
-            nc.tensor.matmul_mx(
-                out=idle[:, HALF - b : HALF] if b == HALF else idle[:, HALF : HALF + b],
-                lhsT=keys[3].bitcast(FP4X4),
-                lhsT_scale=keys["ws"][:, 3 * P : 4 * P],
-                rhs=d_key[:, a:b].bitcast(FP8X4),
-                rhs_scale=planes[:, a:b],
-                start=True,
-                stop=True,
-            )
-        weigh(1, 2, 2)
-        weigh(3, 2, 2)
-        join(2, 2, 1)
-        weave_z(0, 1)
-        join(2, 3, 1)
-        weave_z(1, 1)
-        weigh(2, 2, 1)
-        weigh(2, 3, 1)
-        quant_z(0, 1)
-        weave_z(2, 1)
-        quant_z(1, 1)
-        weave_z(3, 1)
-        quant_z(2, 1)
-        quant_z(3, 1)
-        pieces = [(c, a, a + 2) for c in range(4) for a in (0, 2)]
-        for n, (c, a, b) in enumerate(pieces):
-            piece(n, c, a, b)
-        weave_y(0, 1, nc.vector.tensor_copy, y_half[0][:, :, 0:128])
-        weave_y(1, 1, nc.vector.tensor_copy, y_half[0][:, :, 128:256])
-        weave_y(2, 1, nc.vector.tensor_copy, y_half[1][:, :, 0:128])
+        exp_row(3)
+        invert(1, 2)
+        nc.vector.tensor_scalar(spread[:], gain[:], inv[:, 0:1], None, ALU.mult)
+        make_factor(1, 2)
+        invert(2, 3)
+        pick_vector(0, 0, 2)
+        make_factor(2, 3)
+        invert(3, 4)
+        weigh(0)
+        make_factor(3, 4)
+        weigh(1)
+        weigh(2)
+        weigh(3)
+        pick_vector(0, 2, 1)
+        pick_vector(0, 3, 1)
+        for t in (1, 2, 3):
+            pick_scalar(t, 0, 2)
+        for t in (1, 2, 3):
+            pick_scalar(t, 2, 1)
+        for t in (1, 2, 3):
+            pick_scalar(t, 3, 1)
+        weave_z(0)
+        weave_z(1)
+        quant_z(0)
+        weave_z(2)
+        quant_z(1)
+        quant_z(2)
+        weave_z(3)
+        quant_z(3)
+        for c in range(4):
+            product(c)
+        weave_y(0)
+        weave_y(1)
+        weave_y(2)
         quant_y(0, 2)
         store_codes(0, 2)
-        weave_y(3, 1, nc.vector.tensor_copy, y_half[1][:, :, 128:256])
+        weave_y(3)
         quant_y(2, 1)
         quant_y(3, 1)
         store_codes(2, 2)

@@ -96,10 +96,10 @@ def tile_picked_softkeys_none_po_kernel(
         for h in range(2):
             nc.vector.tensor_copy(x_g[h][:], x_tab[:].indirect(offs_sb[:, 16 * h : 16 * (h + 1)]))
 
-        w_key = sb_at("w_key", [P, 2 * S], U8, 4096)
-        nc.gpsimd.tensor_copy(
-            w_key[:].rearrange("p (t m b) -> p t m b", t=PACK, b=2),
-            w_raw[:].rearrange("p (m t b) -> p t m b", t=PACK, b=2),
+        w_key = sb("w_key", [P, 2 * S], U8)
+        nc.scalar.copy(
+            w_key[:].bitcast(U16).rearrange("p (t c i) -> p c t i", t=PACK, i=8),
+            w_raw[:].bitcast(U16).rearrange("p (c i t) -> p c t i", t=PACK, i=8),
         )
         ws_key = sb_at("ws_key", [P, S], U8, 4096 + 2 * S)
         nc.gpsimd.tensor_copy(
@@ -204,9 +204,9 @@ def tile_picked_softkeys_none_po_kernel(
         def weave_z(c):
             z_words[c] = sb_at("z_words%d" % c, [P, CHUNK * PACK], BF16, 40960 + 1024 * (c % 2))
             nc.vector.tensor_tensor(
-                z_words[c][:].rearrange("p (c t) -> p c t", t=PACK),
-                plain[:, :, CHUNK * c : CHUNK * (c + 1)].rearrange("p t c -> p c t"),
-                picked[c].rearrange("p t c -> p c t"),
+                z_words[c][:].rearrange("p (c i t) -> p c t i", t=PACK, i=4),
+                plain[:, :, CHUNK * c : CHUNK * (c + 1)].rearrange("p t (c i) -> p c t i", i=4),
+                picked[c].rearrange("p t (c i) -> p c t i", i=4),
                 ALU.add,
             )
 

@@ -110,17 +110,16 @@ def tile_picked_softkeys_none_po_kernel(
         first = sb("first", [P, PACK], F32)
         low = sb("low", [P, PACK], F32)
         total = sb("total", [P, PACK], F32)
-        inv = sb("inv", [P, 2], F32)
+        inv = sb("inv", [P, PACK], F32)
         factor = sb("factor", [P, PACK], F32)
         neg = [sb("neg%d" % t, [P, S], F32) for t in range(PACK)]
         win = [sb("win%d" % t, [P, S], F32) for t in range(PACK)]
-        plain = sb_at("plain", [P, PACK, S], F32, 45056)
+        plain_rows = sb_at("plain_rows", [P, PACK * S], F32, 45056)
+        plain = plain_rows[:].rearrange("p (t c) -> p t c", t=PACK)
+        picked = sb("picked", [P, PACK, S], F32)
         gain = sb("gain", [P, HALF], F32)
-        nc.scalar.activation(gain[:], gn32[:, 0:1].to_broadcast([P, HALF]), ACT.Copy)
+        nc.scalar.activation(gain[:], gn32[:, 3:4].to_broadcast([P, HALF]), ACT.Copy)
         spread = sb("spread", [P, HALF], F32)
-        last_inv = sb_at("last_inv", [P, 1], F32, 36864)
-        mid_inv = sb_at("mid_inv", [P, 1], F32, 53248)
-        picked = {}
         z_words = {}
         z_quant = {}
         y_words = {}
@@ -163,42 +162,31 @@ def tile_picked_softkeys_none_po_kernel(
                 win[t][:], neg[t][:], ACT.Exp, bias=low[:, t : t + 1], scale=-1.0, accum_out=total[:, t : t + 1]
             )
 
-        def inverse(a, b):
-            return {0: inv[:, 0:1], 1: mid_inv[:], 2: inv[:, 1:2], 3: last_inv[:]}[a]
-
         def invert(a, b):
-            nc.vector.reciprocal(inverse(a, b), total[:, a:b])
+            nc.vector.reciprocal(inv[:, a:b], total[:, a:b])
 
         def make_factor(a, b):
-            nc.vector.tensor_tensor(factor[:, a:b], inverse(a, b), gn32[:, a:b], ALU.mult)
-
-        def by_row(t):
-            return spread[:, 0:1] if t == 0 else factor[:, t : t + 1]
+            nc.vector.tensor_tensor(factor[:, a:b], inv[:, a:b], gn32[:, a:b], ALU.mult)
 
         def weigh(t):
-            nc.vector.tensor_scalar(plain[:, t, :], win[t][:], by_row(t), None, ALU.mult)
-
-        def slot(t, c, n):
-            if c not in picked:
-                if c == 0:
-                    tile = sb_at("picked0", [P, PACK, HALF], F32, 53248)
-                    picked[0] = tile[:, :, 0:CHUNK]
-                    picked[1] = tile[:, :, CHUNK:HALF]
-                    picked["half"] = tile
-                else:
-                    late = sb_at("picked_late", [P, 2, PACK, CHUNK], F32, 36864)
-                    picked[2] = late[:, 0]
-                    picked[3] = late[:, 1]
-            return picked["half"][:, t, :] if n == 2 else picked[c][:, t, :]
-
-        def pick_scalar(t, c, n):
-            nc.scalar.activation(
-                slot(t, c, n), win[t][:].indirect(nb_sb[:, 8 * c : 8 * (c + n)]), ACT.Copy, scale=by_row(t)
+            nc.vector.tensor_scalar(
+                plain[:, t, :], win[t][:], inv[:, t : t + 1], gn32[:, t : t + 1], ALU.mult, ALU.mult
             )
 
-        def pick_vector(t, c, n):
+        def pick(t, c, n):
+            nc.scalar.activation(
+                picked[:, t, CHUNK * c : CHUNK * (c + n)],
+                win[t][:].indirect(nb_sb[:, 8 * c : 8 * (c + n)]),
+                ACT.Copy,
+                scale=factor[:, t : t + 1],
+            )
+
+        def pick_last(c, n):
             nc.vector.tensor_tensor(
-                slot(t, c, n), win[t][:].indirect(nb_sb[:, 8 * c : 8 * (c + n)]), spread[:, 0 : CHUNK * n], ALU.mult
+                picked[:, 3, CHUNK * c : CHUNK * (c + n)],
+                win[3][:].indirect(nb_sb[:, 8 * c : 8 * (c + n)]),
+                spread[:, 0 : CHUNK * n],
+                ALU.mult,
             )
 
         def weave_z(c):
@@ -206,7 +194,7 @@ def tile_picked_softkeys_none_po_kernel(
             nc.vector.tensor_tensor(
                 z_words[c][:].rearrange("p (c i t) -> p c t i", t=PACK, i=4),
                 plain[:, :, CHUNK * c : CHUNK * (c + 1)].rearrange("p t (c i) -> p c t i", i=4),
-                picked[c].rearrange("p t (c i) -> p c t i", i=4),
+                picked[:, :, CHUNK * c : CHUNK * (c + 1)].rearrange("p t (c i) -> p c t i", i=4),
                 ALU.add,
             )
 
@@ -276,26 +264,22 @@ def tile_picked_softkeys_none_po_kernel(
         invert(0, 1)
         scores(3)
         exp_row(3)
-        invert(1, 2)
-        nc.vector.tensor_scalar(spread[:], gain[:], inv[:, 0:1], None, ALU.mult)
-        make_factor(1, 2)
-        invert(2, 3)
-        pick_vector(0, 0, 2)
-        make_factor(2, 3)
-        invert(3, 4)
+        make_factor(0, 1)
+        invert(1, 3)
         weigh(0)
-        make_factor(3, 4)
+        make_factor(1, 3)
         weigh(1)
+        invert(3, 4)
         weigh(2)
+        nc.vector.tensor_scalar(spread[:], gain[:], inv[:, 3:4], None, ALU.mult)
         weigh(3)
-        pick_vector(0, 2, 1)
-        pick_vector(0, 3, 1)
-        for t in (1, 2, 3):
-            pick_scalar(t, 0, 2)
-        for t in (1, 2, 3):
-            pick_scalar(t, 2, 1)
-        for t in (1, 2, 3):
-            pick_scalar(t, 3, 1)
+        pick_last(0, 2)
+        pick_last(2, 2)
+        for t in range(3):
+            pick(t, 0, 2)
+        for c in (2, 3):
+            for t in range(3):
+                pick(t, c, 1)
         weave_z(0)
         weave_z(1)
         quant_z(0)

@@ -51,20 +51,17 @@ def tile_picked_softkeys_none_po_kernel(
         gn32 = sb("gn32", [P, PACK], F32)
         nc.sync.dma_start(kidx_sb[:], kidx)
         nc.sync.dma_start(offs_sb[:], offs)
+        nc.sync.dma_start(nb_sb[:], nb)
         nc.sync.dma_start(ds_tab[0:P:8, :].bitcast(I32), d_scales[0].bitcast(I32))
         nc.sync.dma_start(xs_tab[0:P:8, :].bitcast(I32), x_scales[0].bitcast(I32))
         nc.sync.dma_start(d_tab[:].bitcast(I32), d_words[0].rearrange("p n t -> p (n t)").bitcast(I32))
         nc.sync.dma_start(x_tab[:].bitcast(I32), x_words[0].rearrange("p n t -> p (n t)").bitcast(I32))
-        nc.sync.dma_start(nb_sb[:], nb)
 
-        ds_g = sb_at("ds_g", [P, S], U8, 1024)
+        ds_g = sb_at("ds_g", [P, S], U8, 1280)
         xs_g = sb_at("xs_g", [P, S], U8, 0)
         planes = sb("planes", [P, 2 * S], U8)
         ds_key = planes[:, 0:S]
         nc.vector.tensor_copy(ds_g[:], ds_tab[:].indirect(kidx_sb[:]))
-        gn_sb = sb_at("gn_sb", [P, PACK], F32, 16384)
-        nc.scalar.dma_start(gn_sb[:], gn.rearrange("(p t) o -> p (t o)", t=PACK))
-        nc.scalar.activation(gn32[:], gn_sb[:], ACT.Copy, scale=32.0)
         nc.vector.tensor_copy(xs_g[:], xs_tab[:].indirect(offs_sb[:]))
         nc.vector.tensor_copy(
             ds_key.rearrange("p (t c i) -> p c t i", t=PACK, i=16),
@@ -73,7 +70,10 @@ def tile_picked_softkeys_none_po_kernel(
         nc.vector.tensor_copy(planes[:, S : 2 * S].bitcast(I32), xs_g[:].bitcast(I32))
         for j in range(1, 4):
             nc.scalar.dma_start(planes[j:P:32, :].bitcast(I32), planes[8 * j : P : 32, :].bitcast(I32))
-        w_raw = sb_at("w_raw", [P, 2 * S], U8, 0)
+        gn_sb = sb_at("gn_sb", [P, PACK], F32, 0)
+        nc.scalar.dma_start(gn_sb[:], gn.rearrange("(p t) o -> p (t o)", t=PACK))
+        nc.scalar.activation(gn32[:], gn_sb[:], ACT.Copy, scale=32.0)
+        w_raw = sb_at("w_raw", [P, 2 * S], U8, 64)
         nc.sync.dma_start(w_raw[:].bitcast(I32), w1_words[0].bitcast(I32))
         d_g = [sb("d_g%d" % h, [P, HALF], U32) for h in range(2)]
         d_key = sb_at("d_key", [P, S], U32, 2048)

@@ -218,17 +218,46 @@ def tile_picked_softkeys_none_po_kernel(
                     start=True,
                     stop=True,
                 )
-            nc.scalar.copy(y_half[h][:, a:b, CHUNK * o : CHUNK * (o + 1)], acc[:])
+            copy = nc.vector.tensor_copy if (c, a) == (2, 2) else nc.scalar.copy
+            copy(y_half[h][:, a:b, CHUNK * o : CHUNK * (o + 1)], acc[:])
             if h == 0:
                 nc.sync.dma_start(
                     out_rows[:, a:b, CHUNK * c : CHUNK * (c + 1)], y_half[0][:, a:b, CHUNK * c : CHUNK * (c + 1)]
                 )
-            elif o == 1:
-                nc.sync.dma_start(out_rows[:, a:b, HALF:S], y_half[1][:, a:b, :])
+            elif b == PACK:
+                nc.sync.dma_start(out_rows[:, :, HALF : HALF + CHUNK], y_half[1][:, :, 0:CHUNK])
 
         def product(c):
             piece(2 * c, c, 0, 2)
             piece(2 * c + 1, c, 2, 4)
+
+        def last_product():
+            codes, scales = z_quant[3]
+            acc = psum.tile([P, PACK, CHUNK], F32, name="acc_last", tag="bank2")
+            for t in range(PACK):
+                nc.tensor.matmul_mx(
+                    out=acc[:, t, :],
+                    lhsT=w_key[:, 2 * P * t : 2 * P * (t + 1)].bitcast(FP4X4),
+                    lhsT_scale=ws_key[:, P * t : P * (t + 1)],
+                    rhs=codes[:].bitcast(FP8X4),
+                    rhs_scale=scales[:],
+                    start=True,
+                    stop=True,
+                )
+            for e in range(2):
+                nc.scalar.copy(y_half[1][:, :, CHUNK + 64 * e : CHUNK + 64 * (e + 1)], acc[:, :, 64 * e : 64 * (e + 1)])
+            nc.sync.dma_start(out_rows[:, :, HALF + CHUNK : S], y_half[1][:, :, CHUNK:HALF])
+
+        def weave_last(e):
+            y_words[3 + e] = sb("y_last%d" % e, [P, 64 * PACK], BF16)[:]
+            nc.vector.tensor_copy(
+                y_words[3 + e].rearrange("p (c i t) -> p c t i", t=PACK, i=4),
+                y_half[1][:, :, CHUNK + 64 * e : CHUNK + 64 * (e + 1)].rearrange("p t (c i) -> p c t i", i=4),
+            )
+
+        def quant_last(e):
+            cols = slice(3 * CHUNK + 64 * e, 3 * CHUNK + 64 * (e + 1))
+            nc.vector.quantize_mx(out=y_codes[:, cols].bitcast(FP8X4), scales=y_scales[:, cols], in_=y_words[3 + e])
 
         def weave_y(c):
             h, o = divmod(c, 2)
@@ -264,10 +293,9 @@ def tile_picked_softkeys_none_po_kernel(
         invert(0, 1)
         scores(3)
         exp_row(3)
-        make_factor(0, 1)
         invert(1, 3)
         weigh(0)
-        make_factor(1, 3)
+        make_factor(0, 3)
         weigh(1)
         invert(3, 4)
         weigh(2)
@@ -288,16 +316,20 @@ def tile_picked_softkeys_none_po_kernel(
         quant_z(2)
         weave_z(3)
         quant_z(3)
-        for c in range(4):
-            product(c)
+        product(0)
         weave_y(0)
+        product(1)
         weave_y(1)
-        weave_y(2)
+        product(2)
+        last_product()
         quant_y(0, 2)
+        weave_y(2)
         store_codes(0, 2)
-        weave_y(3)
         quant_y(2, 1)
-        quant_y(3, 1)
+        weave_last(0)
+        weave_last(1)
+        quant_last(0)
+        quant_last(1)
         store_codes(2, 2)
         for q in range(4):
             queue = nc.scalar if q % 2 == 0 else nc.sync

@@ -96,11 +96,17 @@ def tile_picked_softkeys_none_po_kernel(
         for h in range(2):
             nc.vector.tensor_copy(x_g[h][:], x_tab[:].indirect(offs_sb[:, 16 * h : 16 * (h + 1)]))
 
-        w_key = sb("w_key", [P, 2 * S], U8)
-        nc.scalar.copy(
-            w_key[:].bitcast(U16).rearrange("p (t c i) -> p c t i", t=PACK, i=8),
-            w_raw[:].bitcast(U16).rearrange("p (c i t) -> p c t i", t=PACK, i=8),
-        )
+        keys = {}
+
+        def deal_w(tile, a, b):
+            nc.scalar.copy(
+                tile[:].bitcast(U16).rearrange("p (t c i) -> p c t i", t=b - a, i=8),
+                w_raw[:].bitcast(U16).rearrange("p (c i t) -> p c t i", t=PACK, i=8)[:, :, a:b, :],
+            )
+            for t in range(a, b):
+                keys[t] = tile[:, 2 * P * (t - a) : 2 * P * (t - a + 1)]
+
+        deal_w(sb("w_key", [P, 2 * P * 3], U8), 0, 3)
         ws_key = sb_at("ws_key", [P, S], U8, 4096 + 2 * S)
         nc.gpsimd.tensor_copy(
             ws_key[:].rearrange("p (t c i) -> p c t i", t=PACK, i=16),
@@ -112,7 +118,7 @@ def tile_picked_softkeys_none_po_kernel(
         total = sb("total", [P, PACK], F32)
         inv = sb("inv", [P, PACK], F32)
         factor = sb("factor", [P, PACK], F32)
-        neg = [sb("neg%d" % t, [P, S], F32) for t in range(PACK)]
+        neg = [sb("neg%d" % t, [P, S], F32) for t in range(PACK - 1)] + [sb_at("neg3", [P, S], F32, 32768)]
         win = [sb("win%d" % t, [P, S], F32) for t in range(PACK)]
         plain_rows = sb_at("plain_rows", [P, PACK * S], F32, 45056)
         plain = plain_rows[:].rearrange("p (t c) -> p t c", t=PACK)
@@ -211,7 +217,7 @@ def tile_picked_softkeys_none_po_kernel(
             for t in range(a, b):
                 nc.tensor.matmul_mx(
                     out=acc[:, t - a, :],
-                    lhsT=w_key[:, 2 * P * t : 2 * P * (t + 1)].bitcast(FP4X4),
+                    lhsT=keys[t].bitcast(FP4X4),
                     lhsT_scale=ws_key[:, P * t : P * (t + 1)],
                     rhs=codes[:].bitcast(FP8X4),
                     rhs_scale=scales[:],
@@ -237,7 +243,7 @@ def tile_picked_softkeys_none_po_kernel(
             for t in range(PACK):
                 nc.tensor.matmul_mx(
                     out=acc[:, t, :],
-                    lhsT=w_key[:, 2 * P * t : 2 * P * (t + 1)].bitcast(FP4X4),
+                    lhsT=keys[t].bitcast(FP4X4),
                     lhsT_scale=ws_key[:, P * t : P * (t + 1)],
                     rhs=codes[:].bitcast(FP8X4),
                     rhs_scale=scales[:],
@@ -305,9 +311,23 @@ def tile_picked_softkeys_none_po_kernel(
         pick_last(2, 2)
         for t in range(3):
             pick(t, 0, 2)
-        for c in (2, 3):
-            for t in range(3):
-                pick(t, c, 1)
+        pick(0, 2, 1)
+        pick(1, 2, 1)
+        deal_w(sb_at("w_last", [P, 2 * P], U8, 32768), 3, 4)
+        idle = psum.tile([P, HALF + CHUNK], F32, name="idle", tag="bank3")
+        for a, b in ((0, HALF), (HALF, CHUNK)):
+            nc.tensor.matmul_mx(
+                out=idle[:, a : a + b],
+                lhsT=keys[3].bitcast(FP4X4),
+                lhsT_scale=ws_key[:, 3 * P : 4 * P],
+                rhs=d_key[:, 0:b].bitcast(FP8X4),
+                rhs_scale=planes[:, 0:b],
+                start=True,
+                stop=True,
+            )
+        pick(2, 2, 1)
+        for t in range(3):
+            pick(t, 3, 1)
         weave_z(0)
         weave_z(1)
         quant_z(0)

@@ -32,10 +32,10 @@ def tile_picked_softkeys_none_po_kernel(
         psum = ctx.enter_context(tc.psum_pool(name="psum", bufs=1))
 
         def sb(name, shape, dtype):
-            return keep.tile(shape, dtype, name=name, align_bytes=64)
+            return keep.tile(shape, dtype, name=name, align_bytes=256)
 
         def sb_at(name, shape, dtype, offset):
-            return reuse.tile(shape, dtype, name=name, align_bytes=64, offset=offset)
+            return reuse.tile(shape, dtype, name=name, align_bytes=256, offset=offset)
 
         kidx_sb = sb("kidx_sb", [P, S // 16], U16)
         offs_sb = sb("offs_sb", [P, S // 16], U16)
@@ -73,7 +73,7 @@ def tile_picked_softkeys_none_po_kernel(
         gn_sb = sb_at("gn_sb", [P, PACK], F32, 0)
         nc.scalar.dma_start(gn_sb[:], gn.rearrange("(p t) o -> p (t o)", t=PACK))
         nc.scalar.activation(gn32[:], gn_sb[:], ACT.Copy, scale=32.0)
-        w_raw = sb_at("w_raw", [P, 2 * S], U8, 64)
+        w_raw = sb_at("w_raw", [P, 2 * S], U8, 256)
         nc.sync.dma_start(w_raw[:].bitcast(I32), w1_words[0].bitcast(I32))
         d_g = [sb("d_g%d" % h, [P, HALF], U32) for h in range(2)]
         d_key = sb_at("d_key", [P, S], U32, 2048)

@@ -51,11 +51,14 @@ def tile_picked_softkeys_none_po_kernel(
         gn32 = sb("gn32", [P, PACK], F32)
         nc.sync.dma_start(kidx_sb[:], kidx)
         nc.sync.dma_start(offs_sb[:], offs)
-        nc.sync.dma_start(nb_sb[:], nb)
         nc.sync.dma_start(ds_tab[0:P:8, :].bitcast(I32), d_scales[0].bitcast(I32))
         nc.sync.dma_start(xs_tab[0:P:8, :].bitcast(I32), x_scales[0].bitcast(I32))
         nc.sync.dma_start(d_tab[:].bitcast(I32), d_words[0].rearrange("p n t -> p (n t)").bitcast(I32))
         nc.sync.dma_start(x_tab[:].bitcast(I32), x_words[0].rearrange("p n t -> p (n t)").bitcast(I32))
+        nc.sync.dma_start(nb_sb[:], nb)
+        gn_sb = sb("gn_sb", [P, PACK], F32)
+        nc.sync.dma_start(gn_sb[:], gn.rearrange("(p t) o -> p (t o)", t=PACK))
+        nc.scalar.activation(gn32[:], gn_sb[:], ACT.Copy, scale=32.0)
 
         ds_g = sb_at("ds_g", [P, S], U8, 1280)
         xs_g = sb_at("xs_g", [P, S], U8, 0)
@@ -70,10 +73,7 @@ def tile_picked_softkeys_none_po_kernel(
         nc.vector.tensor_copy(planes[:, S : 2 * S].bitcast(I32), xs_g[:].bitcast(I32))
         for j in range(1, 4):
             nc.scalar.dma_start(planes[j:P:32, :].bitcast(I32), planes[8 * j : P : 32, :].bitcast(I32))
-        gn_sb = sb_at("gn_sb", [P, PACK], F32, 0)
-        nc.scalar.dma_start(gn_sb[:], gn.rearrange("(p t) o -> p (t o)", t=PACK))
-        nc.scalar.activation(gn32[:], gn_sb[:], ACT.Copy, scale=32.0)
-        w_raw = sb_at("w_raw", [P, 2 * S], U8, 256)
+        w_raw = sb_at("w_raw", [P, 2 * S], U8, 0)
         nc.sync.dma_start(w_raw[:].bitcast(I32), w1_words[0].bitcast(I32))
         d_g = [sb("d_g%d" % h, [P, HALF], U32) for h in range(2)]
         d_key = sb_at("d_key", [P, S], U32, 2048)

from contextlib import ExitStack

import concourse.mybir as mybir

F32 = mybir.dt.float32
BF16 = mybir.dt.bfloat16
I32 = mybir.dt.int32
U32 = mybir.dt.uint32
U16 = mybir.dt.uint16
U8 = mybir.dt.uint8
FP8X4 = mybir.dt.float8_e4m3fn_x4
FP4X4 = mybir.dt.float4_e2m1fn_x4
ALU = mybir.AluOpType
ACT = mybir.ActivationFunctionType

P = 128
PACK = 4
TABLE = 2048
S = 512
HALF = 256
CHUNK = 128
FLOPS = 2 * 2 * 512 * 512 * 512


def tile_picked_softkeys_none_po_kernel(
    tc, x_words, x_scales, d_words, d_scales, gn, w1_words, w1_scales, offs, kidx, nb, out_0, out_1, out_2
):
    nc = tc.nc
    with ExitStack() as ctx:
        keep = ctx.enter_context(tc.tile_pool(name="keep", bufs=1))
        reuse = ctx.enter_context(tc.tile_pool(name="reuse", bufs=1))
        psum = ctx.enter_context(tc.psum_pool(name="psum", bufs=1))

        def sb(name, shape, dtype):
            return keep.tile(shape, dtype, name=name, align_bytes=256)

        def sb_at(name, shape, dtype, offset):
            return reuse.tile(shape, dtype, name=name, align_bytes=256, offset=offset)

        kidx_sb = sb("kidx_sb", [P, S // 16], U16)
        offs_sb = sb("offs_sb", [P, S // 16], U16)
        nb_sb = sb("nb_sb", [P, S // 16], U16)
        d_tab = sb_at("d_tab", [P, TABLE], U32, 20480)
        x_tab = sb_at("x_tab", [P, TABLE], U32, 4096)
        ds_tab = sb_at("ds_tab", [P, TABLE], U8, 16384)
        xs_tab = sb("xs_tab", [P, TABLE], U8)

        nc.vector.memset(ds_tab[:].bitcast(I32), 0)
        nc.vector.memset(xs_tab[:].bitcast(I32), 0)

        gn32 = sb("gn32", [P, PACK], F32)
        nc.sync.dma_start(kidx_sb[:], kidx)
        nc.sync.dma_start(offs_sb[:], offs)
        nc.sync.dma_start(ds_tab[0:P:8, :].bitcast(I32), d_scales[0].bitcast(I32))
        nc.sync.dma_start(xs_tab[0:P:8, :].bitcast(I32), x_scales[0].bitcast(I32))
        nc.sync.dma_start(d_tab[:].bitcast(I32), d_words[0].rearrange("p n t -> p (n t)").bitcast(I32))
        nc.sync.dma_start(x_tab[:].bitcast(I32), x_words[0].rearrange("p n t -> p (n t)").bitcast(I32))
        nc.sync.dma_start(nb_sb[:], nb)
        gn_sb = sb("gn_sb", [P, PACK], F32)
        nc.sync.dma_start(gn_sb[:], gn.rearrange("(p t) o -> p (t o)", t=PACK))
        nc.scalar.activation(gn32[:], gn_sb[:], ACT.Copy, scale=32.0)

        ds_g = sb_at("ds_g", [P, S], U8, 1280)
        xs_g = sb_at("xs_g", [P, S], U8, 0)
        planes = sb("planes", [P, 2 * S], U8)
        ds_key = planes[:, 0:S]
        nc.vector.tensor_copy(ds_g[:], ds_tab[:].indirect(kidx_sb[:]))
        nc.vector.tensor_copy(xs_g[:], xs_tab[:].indirect(offs_sb[:]))
        nc.vector.tensor_copy(
            ds_key.rearrange("p (t c i) -> p c t i", t=PACK, i=16),
            ds_g[:].rearrange("p (c i t) -> p c t i", t=PACK, i=16),
        )
        nc.vector.tensor_copy(planes[:, S : 2 * S].bitcast(I32), xs_g[:].bitcast(I32))
        for j in range(1, 4):
            nc.scalar.dma_start(planes[j:P:32, :].bitcast(I32), planes[8 * j : P : 32, :].bitcast(I32))
        w_raw = sb_at("w_raw", [P, 2 * S], U8, 0)
        nc.sync.dma_start(w_raw[:].bitcast(I32), w1_words[0].bitcast(I32))
        d_g = [sb("d_g%d" % h, [P, HALF], U32) for h in range(2)]
        d_key = sb_at("d_key", [P, S], U32, 2048)
        for h in range(2):
            nc.vector.tensor_copy(d_g[h][:], d_tab[:].indirect(kidx_sb[:, 16 * h : 16 * (h + 1)]))

        def deal_keys(h):
            nc.vector.tensor_copy(
                d_key[:].bitcast(I32).rearrange("p (t c i) -> p c t i", t=PACK, i=4)[:, 16 * h : 16 * (h + 1)],
                d_g[h][:].bitcast(I32).rearrange("p (c i t) -> p c t i", t=PACK, i=4),
            )

        deal_keys(0)
        ws_raw = sb_at("ws_raw", [P, S], U8, 20480)
        nc.vector.memset(ws_raw[:].bitcast(I32), 0)
        deal_keys(1)
        for a in range(4):
            nc.sync.dma_start(ws_raw[a:P:32, :].bitcast(I32), w1_scales[0][a:16:4, :].bitcast(I32))
        x_g = [sb("x_g%d" % h, [P, HALF], U32) for h in range(2)]
        for h in range(2):
            nc.vector.tensor_copy(x_g[h][:], x_tab[:].indirect(offs_sb[:, 16 * h : 16 * (h + 1)]))

        keys = {}

        def deal_w(tile, a, b):
            nc.scalar.copy(
                tile[:].bitcast(U16).rearrange("p (t c i) -> p c t i", t=b - a, i=8),
                w_raw[:].bitcast(U16).rearrange("p (c i t) -> p c t i", t=PACK, i=8)[:, :, a:b, :],
            )
            for t in range(a, b):
                keys[t] = tile[:, 2 * P * (t - a) : 2 * P * (t - a + 1)]

        deal_w(sb("w_key", [P, 2 * P * 3], U8), 0, 3)
        ws_key = sb_at("ws_key", [P, S], U8, 4096 + 2 * S)
        nc.gpsimd.tensor_copy(
            ws_key[:].rearrange("p (t c i) -> p c t i", t=PACK, i=16),
            ws_raw[:].rearrange("p (c i t) -> p c t i", t=PACK, i=16),
        )

        first = sb("first", [P, PACK], F32)
        low = sb("low", [P, PACK], F32)
        total = sb("total", [P, PACK], F32)
        inv = sb("inv", [P, PACK], F32)
        factor = sb("factor", [P, PACK], F32)
        neg = [sb("neg%d" % t, [P, S], F32) for t in range(PACK - 1)] + [sb_at("neg3", [P, S], F32, 32768)]
        win = [sb("win%d" % t, [P, S], F32) for t in range(PACK)]
        plain_rows = sb_at("plain_rows", [P, PACK * S], F32, 45056)
        plain = plain_rows[:].rearrange("p (t c) -> p t c", t=PACK)
        picked = sb("picked", [P, PACK, S], F32)
        gain = sb("gain", [P, HALF], F32)
        nc.scalar.activation(gain[:], gn32[:, 3:4].to_broadcast([P, HALF]), ACT.Copy)
        spread = sb("spread", [P, HALF], F32)
        z_words = {}
        z_quant = {}
        y_words = {}
        y_codes = sb("y_codes", [P, S], U32)
        y_scales = sb("y_scales", [P, S], U8)
        y_half = [sb("y_half%d" % h, [P, PACK, HALF], F32) for h in range(2)]
        out_rows = out_0.rearrange("(p t) n -> p t n", t=PACK)
        out_codes = out_1[0].rearrange("p n t -> p (n t)").bitcast(I32)

        def score_pass(out, t, h):
            cols = slice(P * t, P * (t + 1))
            nc.tensor.matmul_mx(
                out=out,
                lhsT=d_key[:, cols].bitcast(FP8X4),
                lhsT_scale=planes[:, cols],
                rhs=x_g[h][:].bitcast(FP8X4),
                rhs_scale=planes[:, S + HALF * h : S + HALF * (h + 1)],
                start=True,
                stop=True,
            )

        def half_scores(t, h):
            score = psum.tile([P, HALF], F32, name="score%d_%d" % (t, h), tag="bank%d" % (t + 4 * h))
            score_pass(score[:], t, h)
            start = first[:, t : t + 1] if h else None
            least = low if h else first
            nc.vector.tensor_scalar(
                neg[t][:, HALF * h : HALF * (h + 1)], score[:], -0.03125, start, ALU.mult, ALU.min,
                accum_out=least[:, t : t + 1],
            )

        def scores(t):
            score = psum.tile([P, S], F32, name="score%d" % t, tag="bank%d" % t)
            for h in range(2):
                score_pass(score[:, HALF * h : HALF * (h + 1)], t, h)
            nc.vector.tensor_scalar(neg[t][:], score[:], -0.03125, None, ALU.mult, ALU.min, accum_out=low[:, t : t + 1])

        def exp_row(t):
            nc.scalar.activation(
                win[t][:], neg[t][:], ACT.Exp, bias=low[:, t : t + 1], scale=-1.0, accum_out=total[:, t : t + 1]
            )

        def invert(a, b):
            nc.vector.reciprocal(inv[:, a:b], total[:, a:b])

        def make_factor(a, b):
            nc.vector.tensor_tensor(factor[:, a:b], inv[:, a:b], gn32[:, a:b], ALU.mult)

        def weigh(t):
            nc.vector.tensor_scalar(
                plain[:, t, :], win[t][:], inv[:, t : t + 1], gn32[:, t : t + 1], ALU.mult, ALU.mult
            )

        def pick(t, c, n):
            nc.scalar.activation(
                picked[:, t, CHUNK * c : CHUNK * (c + n)],
                win[t][:].indirect(nb_sb[:, 8 * c : 8 * (c + n)]),
                ACT.Copy,
                scale=factor[:, t : t + 1],
            )

        def pick_last(c, n):
            nc.vector.tensor_tensor(
                picked[:, 3, CHUNK * c : CHUNK * (c + n)],
                win[3][:].indirect(nb_sb[:, 8 * c : 8 * (c + n)]),
                spread[:, 0 : CHUNK * n],
                ALU.mult,
            )

        def weave_z(c):
            z_words[c] = sb_at("z_words%d" % c, [P, CHUNK * PACK], BF16, 40960 + 1024 * (c % 2))
            nc.vector.tensor_tensor(
                z_words[c][:].rearrange("p (c i t) -> p c t i", t=PACK, i=4),
                plain[:, :, CHUNK * c : CHUNK * (c + 1)].rearrange("p t (c i) -> p c t i", i=4),
                picked[:, :, CHUNK * c : CHUNK * (c + 1)].rearrange("p t (c i) -> p c t i", i=4),
                ALU.add,
            )

        def quant_z(c):
            codes = sb("z_codes%d" % c, [P, CHUNK], U32)
            scales = sb("z_scales%d" % c, [P, CHUNK], U8)
            nc.vector.quantize_mx(out=codes[:].bitcast(FP8X4), scales=scales[:], in_=z_words[c][:])
            z_quant[c] = (codes, scales)

        def piece(n, c, a, b):
            h, o = divmod(c, 2)
            codes, scales = z_quant[c]
            acc = psum.tile([P, b - a, CHUNK], F32, name="acc%d" % n, tag="bank%d" % ((n + 4) % 8))
            for t in range(a, b):
                nc.tensor.matmul_mx(
                    out=acc[:, t - a, :],
                    lhsT=keys[t].bitcast(FP4X4),
                    lhsT_scale=ws_key[:, P * t : P * (t + 1)],
                    rhs=codes[:].bitcast(FP8X4),
                    rhs_scale=scales[:],
                    start=True,
                    stop=True,
                )
            copy = nc.vector.tensor_copy if (c, a) == (2, 2) else nc.scalar.copy
            copy(y_half[h][:, a:b, CHUNK * o : CHUNK * (o + 1)], acc[:])
            if h == 0:
                nc.sync.dma_start(
                    out_rows[:, a:b, CHUNK * c : CHUNK * (c + 1)], y_half[0][:, a:b, CHUNK * c : CHUNK * (c + 1)]
                )
            elif b == PACK:
                nc.sync.dma_start(out_rows[:, :, HALF : HALF + CHUNK], y_half[1][:, :, 0:CHUNK])

        def product(c):
            piece(2 * c, c, 0, 2)
            piece(2 * c + 1, c, 2, 4)

        def last_product():
            codes, scales = z_quant[3]
            acc = psum.tile([P, PACK, CHUNK], F32, name="acc_last", tag="bank2")
            for t in range(PACK):
                nc.tensor.matmul_mx(
                    out=acc[:, t, :],
                    lhsT=keys[t].bitcast(FP4X4),
                    lhsT_scale=ws_key[:, P * t : P * (t + 1)],
                    rhs=codes[:].bitcast(FP8X4),
                    rhs_scale=scales[:],
                    start=True,
                    stop=True,
                )
            for e in range(2):
                nc.scalar.copy(y_half[1][:, :, CHUNK + 64 * e : CHUNK + 64 * (e + 1)], acc[:, :, 64 * e : 64 * (e + 1)])
            nc.sync.dma_start(out_rows[:, :, HALF + CHUNK : S], y_half[1][:, :, CHUNK:HALF])

        def weave_last(e):
            y_words[3 + e] = sb("y_last%d" % e, [P, 64 * PACK], BF16)[:]
            nc.vector.tensor_copy(
                y_words[3 + e].rearrange("p (c i t) -> p c t i", t=PACK, i=4),
                y_half[1][:, :, CHUNK + 64 * e : CHUNK + 64 * (e + 1)].rearrange("p t (c i) -> p c t i", i=4),
            )

        def quant_last(e):
            cols = slice(3 * CHUNK + 64 * e, 3 * CHUNK + 64 * (e + 1))
            nc.vector.quantize_mx(out=y_codes[:, cols].bitcast(FP8X4), scales=y_scales[:, cols], in_=y_words[3 + e])

        def weave_y(c):
            h, o = divmod(c, 2)
            if c == 0:
                y_words["pair"] = sb_at("y_pair", [P, HALF * PACK], BF16, 45056)
            if c < 2:
                y_words[c] = y_words["pair"][:, CHUNK * PACK * c : CHUNK * PACK * (c + 1)]
            else:
                y_words[c] = sb("y_words%d" % c, [P, CHUNK * PACK], BF16)[:]
            nc.vector.tensor_copy(
                y_words[c].rearrange("p (c i t) -> p c t i", t=PACK, i=4),
                y_half[h][:, :, CHUNK * o : CHUNK * (o + 1)].rearrange("p t (c i) -> p c t i", i=4),
            )

        def quant_y(c, n):
            cols = slice(CHUNK * c, CHUNK * (c + n))
            nc.vector.quantize_mx(
                out=y_codes[:, cols].bitcast(FP8X4), scales=y_scales[:, cols], in_=y_words["pair"][:] if n == 2 else y_words[c]
            )

        def store_codes(c, n):
            cols = slice(CHUNK * c, CHUNK * (c + n))
            nc.sync.dma_start(out_codes[:, cols], y_codes[:, cols].bitcast(I32))

        half_scores(0, 0)
        half_scores(1, 0)
        half_scores(0, 1)
        exp_row(0)
        half_scores(1, 1)
        exp_row(1)
        scores(2)
        exp_row(2)
        invert(0, 1)
        scores(3)
        exp_row(3)
        invert(1, 3)
        weigh(0)
        make_factor(0, 3)
        weigh(1)
        invert(3, 4)
        weigh(2)
        nc.vector.tensor_scalar(spread[:], gain[:], inv[:, 3:4], None, ALU.mult)
        weigh(3)
        pick_last(0, 2)
        pick_last(2, 2)
        for t in range(3):
            pick(t, 0, 2)
        pick(0, 2, 1)
        pick(1, 2, 1)
        deal_w(sb_at("w_last", [P, 2 * P], U8, 32768), 3, 4)
        idle = psum.tile([P, HALF + CHUNK], F32, name="idle", tag="bank3")
        for a, b in ((0, HALF), (HALF, CHUNK)):
            nc.tensor.matmul_mx(
                out=idle[:, a : a + b],
                lhsT=keys[3].bitcast(FP4X4),
                lhsT_scale=ws_key[:, 3 * P : 4 * P],
                rhs=d_key[:, 0:b].bitcast(FP8X4),
                rhs_scale=planes[:, 0:b],
                start=True,
                stop=True,
            )
        pick(2, 2, 1)
        for t in range(3):
            pick(t, 3, 1)
        weave_z(0)
        weave_z(1)
        quant_z(0)
        weave_z(2)
        quant_z(1)
        quant_z(2)
        weave_z(3)
        quant_z(3)
        product(0)
        weave_y(0)
        product(1)
        weave_y(1)
        product(2)
        last_product()
        quant_y(0, 2)
        weave_y(2)
        store_codes(0, 2)
        quant_y(2, 1)
        weave_last(0)
        weave_last(1)
        quant_last(0)
        quant_last(1)
        store_codes(2, 2)
        for q in range(4):
            queue = nc.scalar if q % 2 == 0 else nc.sync
            queue.dma_start(out_2[0][4 * q : 4 * q + 4, :].bitcast(I32), y_scales[32 * q : 32 * q + 4, :].bitcast(I32))
